import numpy as np, ml_dtypes
CORES = [16,17,18,19,32,33,34,35]
N = 8
BF = ml_dtypes.bfloat16
V, S, P, Q = 2, 2048, 32, 128
def fill(rng, l, cap):
    l = np.minimum(l, cap); e = S - int(np.sum(l)); o = rng.permutation(P); room = (cap - l)[o]; before = np.add.accumulate(room) - room
    l[o] += np.clip(e - before, 0, room); return l
def lens(rng, cap, g):
    c = np.sort(rng.permutation(S - 1)[:P - 1]) + 1
    return fill(rng, np.diff(np.concatenate([[0], c, [S]])), cap)
def put(d, v, g, a, l):
    j = v % V * P; d["frm"][v // V, g, j:j + P] = a; d["ln"][v // V, g, j:j + P] = l
def make(rng, lengths, share):
    d = {"frm": np.zeros((N, 8, V * P), np.int32), "ln": np.zeros((N, 8, V * P), np.int32), "lit": rng.integers(0, 256, (N, 8, Q)).astype(np.int32)}
    for v in range(N * V):
        for g in range(8):
            s = 1.0 if v == 0 else share[v, g]
            l = lengths(rng, Q if s == 1 else S, g); new = (rng.random(P) < s) & (l <= Q)
            put(d, v, g, np.where(new, S + rng.integers(0, np.maximum(Q - l, 0) + 1), rng.integers(0, S - l + 1)), l)
    return d
def setup_inputs(rng):
    return make(rng, lens, np.full((N * V, 8), 0.25))
def setup_inputs_long(rng):
    def lengths(rng, cap, g):
        l = fill(rng, np.ones(P, np.int64), cap)
        return np.sort(l)[::-1].copy() if g == 0 else np.sort(l) if g == 7 else l
    return make(rng, lengths, np.full((N * V, 8), 0.25))
def setup_inputs_ends(rng):
    d = make(rng, lambda rng, cap, g: np.full(P, S // P), np.full((N * V, 8), 0.25))
    k = rng.integers(0, 3, d["frm"].shape); new = d["frm"] >= S
    d["frm"] = np.where(k == 0, np.where(new, S, 0), np.where(k == 1, np.where(new, S + Q, S) - d["ln"], d["frm"])).astype(np.int32)
    return d
def setup_inputs_moves(rng):
    d = setup_inputs(rng)
    for v in range(1, N * V):
        for g in range(8):
            l = lens(rng, S, g); c = np.add.accumulate(l) - l; p = np.arange(P) if g == v % 8 else rng.permutation(P)
            put(d, v, g, c[p], l[p])
    return d
def setup_inputs_spread(rng):
    share = rng.choice(np.array([0, 0.125, 0.5, 1]), (N * V, 8)); share[N * V - 1, 0] = 0; share[N * V - 1, 1] = 1
    d = make(rng, lambda rng, cap, g: fill(rng, 1 + rng.multinomial(S - P, rng.dirichlet(np.full(P, 0.125))), cap), share)
    d["lit"] = np.where(rng.random(d["lit"].shape) < 0.5, 255 * rng.integers(0, 2, d["lit"].shape), d["lit"]).astype(np.int32)
    return d
def check_inputs(d):
    bad = []; a = np.asarray(d["frm"]).astype(np.int64).reshape(N, 8, V, P); l = np.asarray(d["ln"]).astype(np.int64).reshape(N, 8, V, P); t = np.asarray(d["lit"])
    if (l < 1).any() or (np.sum(l, axis=3) != S).any(): bad.append("lengths")
    copied = (a >= 0) & (a + l <= S); new = (a >= S) & (a + l <= S + Q)
    if not (copied | new).all(): bad.append("pieces")
    if not new[0, :, 0].all(): bad.append("version 0")
    if (t < 0).any() or (t > 255).any(): bad.append("literals")
    return bad
def reference(frm, ln, lit):
    y = np.zeros((N, 8, V * S), np.float32); old = np.zeros((8, S), np.int64)
    for v in range(N * V):
        r, k = v // V, v % V; src = np.concatenate([old, lit[r]], axis=1); new = np.zeros((8, S), np.int64)
        for g in range(8):
            a = frm[r, g, k * P:(k + 1) * P]; l = ln[r, g, k * P:(k + 1) * P]; first = np.add.accumulate(l) - l
            new[g] = src[g][np.repeat(a - first, l) + np.arange(S)]
        y[r, :, k * S:(k + 1) * S] = new; old = new
    return {"y": y}

@@ -1,0 +1,359 @@
+from concourse.bass import DstId, RemoteDMATransfer
+from concourse.mybir import AluOpType as OP, ActivationFunctionType as AF
+
+ID, S1, S2, S3, S4, WEND = 0, 2176, 4352, 6528, 8704, 10880
+Y3, Y7, Y11, YF, YEND = 0, 2432, 4864, 7296, 9344
+SYM = 2176
+SCRATCH = {
+    "stage": ("dram", [8, 128, 2], "int32"), "land": ("dram", [8, 128, 2], "int32"),
+    "ost": ("dram", [8, 128, 32], "float32"), "yland": ("dram", [8, 128, 32], "float32"),
+    "fr": ("sbuf", [128, 32], "int32"), "ln2": ("sbuf", [128, 32], "int32"), "litr": ("sbuf", [128, 128], "int32"),
+    "lnf": ("sbuf", [128, 40], "float32"), "hf": ("sbuf", [128, 40], "float32"),
+    "first": ("sbuf", [128, 32], "float32"), "dr": ("sbuf", [128, 32], "float32"), "ones": ("sbuf", [128, 32], "float32"),
+    "id16": ("sbuf", [128, 16], "float32"), "pint": ("sbuf", [128, 8], "int32"), "pf": ("sbuf", [128, 16], "float32"),
+    "xi": ("sbuf", [128, 8], "int32"), "zi": ("sbuf", [128, 24], "int32"), "zf": ("sbuf", [128, 32], "float32"),
+    "cb": ("sbuf", [128, 128 * 96], "bfloat16"),
+    "W": ("sbuf", [128, WEND], "float32"), "Y": ("sbuf", [128, YEND], "float32"), "O": ("sbuf", [128, 2048], "float32"),
+    "lr": ("sbuf", [128, 128], "float32"),
+}
+for _n in ("l0", "l5", "l6", "l7"):
+    SCRATCH["f" + _n] = ("sbuf", [128, 128], "float32")
+for _n in ("1", "2", "3", "4", "0", "5", "6", "7"):
+    SCRATCH["u" + _n] = ("sbuf", [128, 128], "uint16")
+for _n in ("p1", "p2", "p3", "p4", "p0", "px", "pta", "ptb"):
+    SCRATCH[_n] = ("psum", [128, 512], "float32")
+SEMAPHORES = ["cv", "ca", "cp", "cg", "ld", "own", "arr", "lfr", "llit", "dl0", "dy3", "dl5", "dl6", "dl7",
+              "sh0", "sh1", "sh2", "sh3", "shown", "rloc", "yarr", "yst"]
+CALLS = [[0, 1], [3], [2, 4, 5], [6, 7]]
+
+
+def engines_of(r):
+    for grp in CALLS:
+        if r in grp:
+            n = 2 if len(grp) == 3 else 4
+            k = grp.index(r)
+            return k * n, k * n + n
+
+
+def rank_program(g, core, T, topo):
+    me = T.rank_of(core)
+    if me is None:
+        return
+    eng = {"v": g.vector, "a": g.scalar, "p": g.tensor, "g": g, "s": g.sync}
+    cnt, seen, slots = {}, {}, {}
+
+    def need(q, toks):
+        for sem, val in toks:
+            if seen.get((q, sem), 0) < val:
+                eng[q].wait_ge(T.sem[sem], val)
+                seen[(q, sem)] = val
+
+    def tok(ins, sem, n=1):
+        cnt[sem] = cnt.get(sem, 0) + n
+        ins.then_inc(T.sem[sem], n)
+        return (sem, cnt[sem])
+
+    def al(*sems):
+        return [(s, cnt[s]) for s in sems]
+
+    def dma(q, out, in_, sem, toks=()):
+        need(q, toks)
+        return tok(eng[q].dma_start(out=out, in_=in_), sem, 16)
+
+    def C(name):
+        if name not in slots:
+            slots[name] = len(slots)
+        k = slots[name]
+        return T.cb[:, 128 * k:128 * k + 128]
+
+    def Cs(name, p1, c0, c1):
+        C(name)
+        k = 128 * slots[name]
+        return T.cb[0:p1, k + c0:k + c1]
+
+    def ts(out, a, s1, s2, o0, o1=None, toks=()):
+        need("v", toks)
+        if o1 is None:
+            return tok(g.vector.tensor_scalar(out, a, s1, None, o0), "cv")
+        return tok(g.vector.tensor_scalar(out, a, s1, s2, o0, o1), "cv")
+
+    def tt(out, a, b, op, toks=()):
+        need("v", toks)
+        return tok(g.vector.tensor_tensor(out, a, b, op), "cv")
+
+    def cp(out, a, toks=()):
+        need("v", toks)
+        return tok(g.vector.tensor_copy(out, a), "cv")
+
+    def ms(out, x):
+        return tok(g.vector.memset(out, x), "cv")
+
+    def act(out, a, toks=(), **kw):
+        need("a", toks)
+        if kw:
+            return tok(g.scalar.activation(out, a, AF.Identity, **kw), "ca")
+        return tok(g.scalar.activation(out, a, AF.Copy), "ca")
+
+    def iota(out, pattern, base, ch):
+        return tok(g.iota(out, pattern, base, ch, allow_small_or_imprecise_dtypes=True), "cg")
+
+    def mms(out, pairs, start, stop, toks):
+        need("p", toks)
+        for n, (l, r) in enumerate(pairs):
+            ins = g.tensor.matmul(out, l, r, start and n == 0, stop and n == len(pairs) - 1)
+        return tok(ins, "cp")
+
+    dma("s", T.stage[:, 0:32, :], T.frm[:, :], "ld")
+    dma("a", T.stage[:, 32:64, :], T.ln[:, :], "ld")
+    dma("s", T.stage[:, 64:128, :], T.lit[:, :], "ld")
+    dma("a", T.land[me:me + 1, 0:32, :], T.frm[me:me + 1, :], "own")
+    dma("s", T.land[me:me + 1, 32:64, :], T.ln[me:me + 1, :], "own")
+    dma("a", T.land[me:me + 1, 64:128, :], T.lit[me:me + 1, :], "own")
+    kp = iota(T.pint[:, 0:1], [[0, 1]], 0, 1)
+    k1 = iota(C("ac"), [[0, 16], [16, 8]], 0, 0)
+    k2 = iota(C("key"), [[1, 16], [16, 8]], 0, 0)
+    k3 = iota(C("cc"), [[1, 128]], 0, 0)
+    need("g", al("ld"))
+    trs = []
+    for r in range(8):
+        if r != me:
+            rid, pid = topo.addr(T.cores[r])[:2]
+            e = topo.engines(core, T.cores[r])
+            trs.append(RemoteDMATransfer(dst_ids=[DstId(rid=rid, pnc=pid)], dma_engine_mask=1 << e[len(trs)],
+                                         remote_sem=T.sem.arr, src=T.stage[r], dst=T.land[me]))
+    g.remote_dma_fused(trs, local_sem=T.sem.rloc)
+    cnt["rloc"] = 7
+    cnt["arr"] = 7
+    k4 = iota(C("grp"), [[1, 8], [0, 16]], 0, 0)
+    k5 = iota(C("gb2"), [[2, 4], [0, 32]], 0, 0)
+    k6 = iota(C("dm"), [[1, 128]], 0, -1)
+    kid = iota(T.W[:, 0:512], [[1, 512]], 0, 0)
+
+    need("s", al("arr", "own"))
+    dma("s", T.fr[0:16, :], T.land[:, 0:32, :], "lfr")
+    dma("s", T.ln2[0:16, :], T.land[:, 32:64, :], "lfr")
+    dma("s", T.litr[0:8, :], T.land[:, 64:128, :], "llit")
+
+    ms(T.lnf[:, 0:1], 0.0)
+    ms(T.hf[:, 0:1], 0.0)
+    ms(T.ones[:, :], 1.0)
+    ms(T.fl7[0:64, :], 0.0)
+    ms(C("ma0"), 0.0)
+    ms(C("ia0"), 0.0)
+    ms(C("zero"), 0.0)
+    my3 = ms(T.Y[:, Y3:Y3 + 2176], 0.0)
+    a1 = ts(T.pint[:, 1:2], T.pint[:, 0:1], 15, None, OP.bitwise_and, None, [kp])
+    a2 = ts(T.pint[:, 2:3], T.pint[:, 0:1], 5, None, OP.logical_shift_right)
+    a3 = ts(T.pint[:, 3:4], T.pint[:, 0:1], 4, 1, OP.logical_shift_right, OP.bitwise_and)
+    c1 = tt(C("cd"), C("key"), C("ac"), OP.subtract, [k3])
+    c2 = ts(C("phl"), C("ac"), 16.0, None, OP.mult)
+    b1 = cp(T.pf[:, 0:4], T.pint[:, 0:4], [a3])
+    c3 = ts(C("phn"), C("cd"), 128.0, None, OP.mult, None, [c1])
+    g16 = ts(C("g16"), C("grp"), 16.0, None, OP.mult, None, [k4])
+    ts(T.pf[:, 4:5], T.pf[:, 2:3], 2.0, None, OP.mult, None, [b1])
+    ts(T.pf[:, 6:7], T.pf[:, 2:3], 2.0, 1.0, OP.mult, OP.add)
+    ts(T.pf[:, 5:6], T.pf[:, 1:2], 16.0, None, OP.mult)
+    ts(T.pf[:, 7:8], T.pf[:, 3:4], 0.0, None, OP.is_equal)
+    ts(T.pf[:, 8:9], T.pf[:, 0:1], 32.0, 2176.0, OP.is_ge, OP.mult)
+    ts(T.pf[:, 9:10], T.pf[:, 3:4], 0.0, 2176.0, OP.is_equal, OP.mult)
+    b2 = ts(T.pf[:, 10:11], T.pf[:, 0:1], 16.0, 2432.0, OP.is_ge, OP.mult)
+    mm = tt(C("mm"), C("cc"), C("g16"), OP.subtract, [g16])
+    ident = ts(C("id"), C("dm"), 0.0, None, OP.is_equal, None, [k6])
+    ts(C("pln"), C("ac"), T.pf[:, 1:2], None, OP.add, None, [b2])
+    ts(C("pll"), C("cd"), T.pf[:, 5:6], None, OP.add)
+    ts(C("ma"), C("grp"), T.pf[:, 4:5], None, OP.is_equal)
+    mb = ts(C("mb"), C("grp"), T.pf[:, 6:7], None, OP.is_equal)
+    ts(C("m1"), C("mm"), 1.0, None, OP.add, None, [mm])
+    ts(C("m99"), C("mm"), -99.0, None, OP.add)
+    tt(C("mall"), C("ma"), C("mb"), OP.add, [mb])
+    cp(Cs("ma0", 128, 0, 16), Cs("ma", 128, 0, 16))
+    x = tt(C("ma1"), C("ma"), C("ma0"), OP.subtract, al("cv"))
+    ts(C("ia"), C("id"), T.pf[:, 7:8], None, OP.mult)
+    ts(C("ib"), C("id"), T.pf[:, 3:4], None, OP.mult)
+    cp(Cs("ia0", 128, 0, 16), Cs("id", 128, 0, 16))
+    cp(T.id16[0:16, :], Cs("id", 16, 0, 16))
+    x = tt(C("ir"), C("id"), C("ia0"), OP.subtract, al("cv"))
+    for n in ("all", "a0", "b", "a1"):
+        x = tt(C("g" + n), C("m1"), C("m" + n), OP.mult)
+    for n in ("b", "a1"):
+        x = tt(C("s" + n), C("m99"), C("m" + n), OP.mult)
+    need("v", al("cv"))
+    for n in ("all", "a0", "b", "a1"):
+        ts(C("G" + n), C("g" + n), -1.0, None, OP.add)
+    for n in ("b", "a1"):
+        ts(C("L" + n), C("s" + n), 99.0, None, OP.add)
+    ts(Cs("sel0", 8, 0, 128), Cs("gb2", 8, 0, 128), T.pf[0:8, 0:1], None, OP.is_equal, None, [k5])
+    ts(Cs("sel1", 8, 0, 128), Cs("gb2", 8, 0, 128), 1.0, T.pf[0:8, 0:1], OP.add, OP.is_equal)
+    for r in (2, 4, 6):
+        setup = ts(Cs("r%d" % r, 8, 0, 128), Cs("zero", 8, 0, 128), T.pf[0:8, 0:1], float(r), OP.add, OP.is_equal)
+
+    i1 = act(T.W[:, 512:1024], T.W[:, 0:512], [kid], bias=512.0)
+    i2 = act(T.W[:, 1024:2048], T.W[:, 0:1024], [i1], bias=1024.0)
+    for y in (Y3, Y7, Y11):
+        act(T.Y[:, y + SYM:y + SYM + 256], T.W[:, 0:256])
+
+    P = {n: T["p%d" % n][:, 0:128] for n in (0, 1, 2, 3, 4)}
+    for n in (1, 2, 3):
+        mms(P[n], [(C("id"), C("phn")), (C("id"), C("pln"))], True, False, [setup])
+    mms(P[4], [(C("ia0"), C("phn")), (C("ia0"), C("pln")), (C("ir"), C("phl")), (C("ir"), C("pll"))], True, False, [])
+    mms(P[0], [(C("ib"), C("phl")), (C("ib"), C("pll"))], True, False, [])
+
+    n1 = cp(T.lnf[0:16, 1:33], T.ln2[0:16, :], al("lfr"))
+    n2 = tt(T.hf[0:16, 1:33], T.fr[0:16, :], T.ln2[0:16, :], OP.add)
+    need("v", [n1])
+    n3 = tok(g.vector.tensor_tensor_scan(T.first[0:16, :], T.lnf[0:16, 0:32], T.ones[0:16, :], 0.0, OP.add, OP.mult), "cv")
+    n4 = tt(T.dr[0:16, :], T.fr[0:16, :], T.hf[0:16, 0:32], OP.subtract, [n2])
+    nl = cp(Cs("lit", 8, 0, 128), T.litr[0:8, :], al("llit"))
+    for q, (buf, t) in enumerate(((T.first, n3), (T.dr, n4))):
+        need("p", [t])
+        for b in range(4):
+            ins = g.tensor.matmul(T.px[32 * b:32 * b + 32, 4 * q:4 * q + 4], buf[0:16, 0:32], T.id16[0:16, 4 * b:4 * b + 4], True, True)
+    tx = tok(ins, "cp")
+    need("p", [nl])
+    for k, n in enumerate(("sel0", "sel1", "r2", "r4")):
+        ins = g.tensor.matmul(T.pta[:, 128 * k:128 * k + 128], Cs(n, 8, 0, 128), Cs("lit", 8, 0, 128), True, True)
+    tta = tok(ins, "cp")
+    ttb = tok(g.tensor.matmul(T.ptb[:, 0:128], Cs("r6", 8, 0, 128), Cs("lit", 8, 0, 128), True, True), "cp")
+    code = T.pf[:, 8:9]
+    act(T.W[:, ID + 2048:ID + 2176], T.pta[:, 0:128], [tta, b2], bias=code)
+    act(T.W[:, S1 + 2048:S1 + 2176], T.pta[:, 0:128], bias=code)
+    act(T.W[:, S2 + 2048:S2 + 2176], T.pta[:, 128:256], bias=code)
+    tails = act(T.W[:, S3 + 2048:S3 + 2176], T.pta[:, 128:256], bias=code)
+
+    x = cp(T.xi[:, :], T.px[:, 0:8], [tx])
+    ts(T.zi[:, 0:4], T.xi[:, 0:4], 15, None, OP.bitwise_and, None, [x])
+    zh = ts(T.zi[:, 4:8], T.xi[:, 0:4], 4, None, OP.logical_shift_right)
+    ts(T.zi[:, 8:12], T.xi[:, 4:8], -64, None, OP.bitwise_and)
+    x = ts(T.zi[:, 12:16], T.xi[:, 4:8], 63, None, OP.bitwise_and)
+    zz = cp(T.zf[:, 0:16], T.zi[:, 0:16], [x])
+
+    def Z(k, t):
+        return T.zf[:, 4 * k + t:4 * k + t + 1]
+
+    def nat(n, t, m, toks, stop):
+        need("v", toks)
+        w = "%d%s" % (t, n)
+        for h in (0, 1):
+            ts(C("n1" + w + str(h)), C("cc"), Z(1, t), Z(2 + h, t), OP.is_gt, OP.mult)
+        for h in (0, 1):
+            ts(C("n2" + w + str(h)), C("cc"), Z(1, t), Z(2 + h, t), OP.is_equal, OP.mult)
+        x = ts(C("nl" + w), C("G" + m), Z(0, t), None, OP.is_ge)
+        return mms(P[n], [(C("m" + m), C("n1" + w + str(h))) for h in (0, 1)] +
+                   [(C("nl" + w), C("n2" + w + str(h))) for h in (0, 1)], False, stop, [x])
+
+    def lst(n, t, m, toks, stop):
+        need("v", toks)
+        w = "%d%s" % (t, n)
+        pr = []
+        for k, (row, z, op, side, lop) in enumerate((("ac", 5, OP.is_gt, "L", OP.is_lt), ("ac", 5, OP.is_ge, "G", OP.is_gt),
+                                                     ("key", 6, OP.is_ge, "G", OP.is_equal))):
+            for h in (0, 1):
+                ts(C("q%d%s%d" % (k, w, h)), C(row), Z(z, t), Z(2 + h, t), op, OP.mult)
+            x = ts(C("ql%d%s" % (k, w)), C(side + m), Z(4, t), None, lop)
+            pr += [(C("ql%d%s" % (k, w)), C("q%d%s%d" % (k, w, h))) for h in (0, 1)]
+        return mms(P[n], pr, False, stop, [x])
+
+    def gather(out, o0, win, w0, w1, lu, nv, toks, pre=()):
+        need("v", toks)
+        tv = tok(g.vector.tensor_copy(out[:, o0:o0 + 16 * nv], win[:, w0:w1].indirect(lu[:, 0:nv])), "cv")
+        need("a", toks)
+        ta = tok(g.scalar.activation(out[:, o0 + 16 * nv:o0 + 2048], win[:, w0:w1].indirect(lu[:, nv:128]), AF.Copy), "ca")
+        return [tv, ta]
+
+    def ship(v, src, sem, toks):
+        r, k = v // 2, v % 2
+        if r == me:
+            dma("s", T.y[me:me + 1, 2048 * k:2048 * k + 2048], src, "shown", toks)
+        else:
+            dma("s", T.ost[r:r + 1, 64 * k:64 * k + 64, :], src, sem, toks)
+
+    def ship2(r, src, sem, toks, q="s"):
+        if r == me:
+            dma(q, T.y[me:me + 1, :], src, "shown", toks)
+        else:
+            dma(q, T.ost[r:r + 1, :, :], src, sem, toks)
+
+    def send(c):
+        trs = []
+        for r in CALLS[c]:
+            if r != me:
+                rid, pid = topo.addr(T.cores[r])[:2]
+                a, b = engines_of(r)
+                m = 0
+                for e in topo.engines(core, T.cores[r])[a:b]:
+                    m |= 1 << e
+                trs.append(RemoteDMATransfer(dst_ids=[DstId(rid=rid, pnc=pid)], dma_engine_mask=m,
+                                             remote_sem=T.sem.yarr, src=T.ost[r], dst=T.yland[me]))
+                cnt["rloc"] += b - a
+        if trs:
+            need("g", al("sh%d" % c))
+            g.remote_dma_fused(trs, local_sem=T.sem.rloc)
+
+    t1 = nat(1, 0, "all", [zz, setup], True)
+    e1 = cp(T.u1[:, :], T.p1[:, 0:128], [t1])
+    t2 = nat(2, 1, "all", [], True)
+    s1 = gather(T.W, S1, T.W, ID, ID + 2176, T.u1, 52, [e1, i2, tails])
+    e2 = cp(T.u2[:, :], T.p2[:, 0:128], [t2])
+    elr = act(T.lr[:, :], T.p1[:, 0:128], [e1])
+    dma("s", T.fl0[0:16, :], T.lr[32:48, :], "dl0", [elr])
+    dma("s", T.fl6[16:32, :], T.lr[64:80, :], "dl6")
+    dma("s", T.fl7[64:80, :], T.lr[96:112, :], "dl7")
+    ship(0, T.W[0:1, S1:S1 + 2048], "sh0", s1)
+    t3 = nat(3, 2, "all", [], True)
+    ts(T.zi[:, 16:20], T.zi[:, 4:8], 15, None, OP.bitwise_and, None, [zh])
+    x = ts(T.zi[:, 20:24], T.zi[:, 4:8], 112, None, OP.bitwise_and)
+    x = cp(T.zf[:, 16:24], T.zi[:, 16:24], [x])
+    zl = tt(T.zf[:, 24:28], T.zf[:, 20:24], T.zf[:, 0:4], OP.add, [x])
+    s2 = gather(T.W, S2, T.W, S1, S1 + 2176, T.u2, 50, s1 + [e2])
+    e3 = cp(T.u3[:, :], T.p3[:, 0:128], [t3])
+    ship(1, T.W[0:1, S2:S2 + 2048], "sh0", s2)
+    act(T.W[:, S4 + 2048:S4 + 2176], T.pta[:, 256:384])
+    nat(4, 3, "a0", [zl], False)
+    lst(4, 3, "a1", [], False)
+    s3 = gather(T.W, S3, T.W, S2, S2 + 2176, T.u3, 46, s2 + [e3])
+    act(T.Y[:, Y7 + 2048:Y7 + 2176], T.pta[:, 384:512])
+    t4 = lst(4, 2, "b", [], True)
+    e4 = ts(T.u4[:, :], T.p4[:, 0:128], T.pf[:, 9:10], None, OP.add, None, [t4])
+    ship(2, T.W[0:1, S3:S3 + 2048], "sh0", s3)
+    s4 = gather(T.W, S4, T.W, S2, S3 + 2176, T.u4, 60, s3 + [e4])
+    rows = T.W
+    dma("s", T.Y[0:128:16, Y3:Y3 + 2048], rows[0:8, S4:S4 + 2048], "dy3", s4 + [my3])
+    dma("a", T.fl5[16:128, :], rows[32:39, S4:S4 + 2048], "dl5", s4)
+    dma("s", T.fl5[0:16, :], rows[48:49, S4:S4 + 2048], "dl5")
+    dma("s", T.fl6[64:128, :], rows[64:68, S4:S4 + 2048], "dl6")
+    dma("s", T.fl6[48:64, :], rows[80:81, S4:S4 + 2048], "dl6")
+    dma("s", T.fl7[96:112, :], rows[112:113, S4:S4 + 2048], "dl7", [setup])
+    dma("s", T.fl7[112:128, :], rows[96:97, S4:S4 + 2048], "dl7")
+    ship(3, T.W[0:1, S4:S4 + 2048], "sh0", s4)
+    t0 = lst(0, 1, "b", [], True)
+    x = cp(T.u0[:, :], T.p0[:, 0:128], [t0])
+    e0 = ts(T.u0[0:16, :], T.fl0[0:16, :], float(S4 - S1), None, OP.add, None, al("dl0") + [x])
+    s0 = gather(T.O, 0, T.W, S1, S4 + 2176, T.u0, 54, s4 + [e0])
+    act(T.Y[:, Y11 + 2048:Y11 + 2176], T.ptb[:, 0:128], [ttb])
+    dma("s", T.fl6[0:16, :], T.O[48:49, :], "dl6", s0)
+    dma("s", T.fl6[32:48, :], T.O[80:81, :], "dl6")
+    dma("s", T.fl7[80:96, :], T.O[112:113, :], "dl7")
+    ship(4, T.O[0:1, :], "sh2", s0)
+    e5 = cp(T.u5[:, :], T.fl5[:, :], al("dl5"))
+    s5 = gather(T.Y, Y7, T.Y, Y3, Y3 + 2432, T.u5, 64, al("dy3") + [e5])
+    ship2(3, T.Y[0:32:16, Y7:Y7 + 2048], "sh1", s5)
+    e6 = ts(T.u6[:, :], T.fl6[:, :], T.pf[:, 10:11], None, OP.add, None, al("dl6"))
+    s6 = gather(T.Y, Y11, T.Y, Y3, Y7 + 2432, T.u6, 64, s5 + [e6])
+    ship2(4, T.Y[16:48:16, Y11:Y11 + 2048], "sh2", s6)
+    ship2(5, T.Y[48:80:16, Y11:Y11 + 2048], "sh2", s6)
+    ship(5, T.Y[0:1, Y11:Y11 + 2048], "sh2", s6)
+    e7 = cp(T.u7[:, :], T.fl7[:, :], al("dl7"))
+    s7 = gather(T.Y, YF, T.Y, Y11, Y11 + 2432, T.u7, 64, s6 + [e7])
+    ship2(6, T.Y[64:96:16, YF:YF + 2048], "sh3", s7)
+    ship2(7, T.Y[96:128:16, YF:YF + 2048], "sh3", s7, "a")
+    for c in range(4):
+        send(c)
+    a, b = engines_of(me)
+    cnt["yarr"] = 7 * (b - a)
+    if me > 0:
+        dma("s", T.y[0:me, :], T.yland[0:me, :, :], "yst", al("yarr"))
+    if me < 7:
+        dma("a", T.y[me + 1:8, :], T.yland[me + 1:8, :, :], "yst", al("yarr"))
+    for s in list(cnt):
+        if max([v for (q, n), v in seen.items() if n == s] + [0]) < cnt[s]:
+            need("g", [(s, cnt[s])])

@@ -4,15 +4,17 @@ from concourse.mybir import AluOpType as OP, ActivationFunctionType as AF
 ID, S1, S2, S3, S4, WEND = 0, 2176, 4352, 6528, 8704, 10880
 Y3, Y7, Y11, YF, YEND = 0, 2432, 4864, 7296, 9344
 SYM = 2176
+NV = [44, 42, 42, 62, 64, 64, 64, 64]
 SCRATCH = {
     "stage": ("dram", [8, 128, 2], "int32"), "land": ("dram", [8, 128, 2], "int32"),
     "ost": ("dram", [8, 128, 32], "float32"), "yland": ("dram", [8, 128, 32], "float32"),
     "fr": ("sbuf", [128, 32], "int32"), "ln2": ("sbuf", [128, 32], "int32"), "litr": ("sbuf", [128, 128], "int32"),
     "lnf": ("sbuf", [128, 40], "float32"), "hf": ("sbuf", [128, 40], "float32"),
-    "first": ("sbuf", [128, 32], "float32"), "dr": ("sbuf", [128, 32], "float32"), "ones": ("sbuf", [128, 32], "float32"),
-    "id16": ("sbuf", [128, 16], "float32"), "pint": ("sbuf", [128, 8], "int32"), "pf": ("sbuf", [128, 16], "float32"),
-    "xi": ("sbuf", [128, 8], "int32"), "zi": ("sbuf", [128, 24], "int32"), "zf": ("sbuf", [128, 32], "float32"),
-    "cb": ("sbuf", [128, 128 * 96], "bfloat16"),
+    "first": ("sbuf", [128, 32], "float32"), "ones": ("sbuf", [128, 32], "float32"),
+    "fi": ("sbuf", [128, 32], "int32"), "di": ("sbuf", [128, 32], "int32"),
+    "qi": ("sbuf", [128, 224], "int32"), "qb": ("sbuf", [128, 224], "bfloat16"),
+    "pint": ("sbuf", [128, 8], "int32"), "pf": ("sbuf", [128, 16], "float32"), "zf": ("sbuf", [128, 16], "float32"),
+    "ci": ("sbuf", [128, 512], "int32"), "cb": ("sbuf", [128, 128 * 96], "bfloat16"),
     "W": ("sbuf", [128, WEND], "float32"), "Y": ("sbuf", [128, YEND], "float32"), "O": ("sbuf", [128, 2048], "float32"),
     "lr": ("sbuf", [128, 128], "float32"),
 }
@@ -20,7 +22,7 @@ for _n in ("l0", "l5", "l6", "l7"):
     SCRATCH["f" + _n] = ("sbuf", [128, 128], "float32")
 for _n in ("1", "2", "3", "4", "0", "5", "6", "7"):
     SCRATCH["u" + _n] = ("sbuf", [128, 128], "uint16")
-for _n in ("p1", "p2", "p3", "p4", "p0", "px", "pta", "ptb"):
+for _n in ("p1", "p2", "p3", "p4", "px", "pta", "ptb"):
     SCRATCH[_n] = ("psum", [128, 512], "float32")
 SEMAPHORES = ["cv", "ca", "cp", "cg", "ld", "own", "arr", "lfr", "llit", "dl0", "dy3", "dl5", "dl6", "dl7",
               "sh0", "sh1", "sh2", "sh3", "shown", "rloc", "yarr", "yst"]
@@ -110,9 +112,10 @@ def rank_program(g, core, T, topo):
     dma("s", T.land[me:me + 1, 32:64, :], T.ln[me:me + 1, :], "own")
     dma("a", T.land[me:me + 1, 64:128, :], T.lit[me:me + 1, :], "own")
     kp = iota(T.pint[:, 0:1], [[0, 1]], 0, 1)
-    k1 = iota(C("ac"), [[0, 16], [16, 8]], 0, 0)
-    k2 = iota(C("key"), [[1, 16], [16, 8]], 0, 0)
-    k3 = iota(C("cc"), [[1, 128]], 0, 0)
+    kc = iota(T.ci[:, 0:128], [[1, 128]], 0, 0)
+    ka = iota(C("ac"), [[0, 16], [16, 8]], 0, 0)
+    kk = iota(C("key"), [[1, 16], [16, 8]], 0, 0)
+    kid = iota(T.W[:, 0:256], [[1, 256]], 0, 0)
     need("g", al("ld"))
     trs = []
     for r in range(8):
@@ -124,136 +127,146 @@ def rank_program(g, core, T, topo):
     g.remote_dma_fused(trs, local_sem=T.sem.rloc)
     cnt["rloc"] = 7
     cnt["arr"] = 7
-    k4 = iota(C("grp"), [[1, 8], [0, 16]], 0, 0)
-    k5 = iota(C("gb2"), [[2, 4], [0, 32]], 0, 0)
-    k6 = iota(C("dm"), [[1, 128]], 0, -1)
-    kid = iota(T.W[:, 0:512], [[1, 512]], 0, 0)
 
     need("s", al("arr", "own"))
-    dma("s", T.fr[0:16, :], T.land[:, 0:32, :], "lfr")
     dma("s", T.ln2[0:16, :], T.land[:, 32:64, :], "lfr")
+    dma("s", T.fr[0:16, :], T.land[:, 0:32, :], "lfr")
     dma("s", T.litr[0:8, :], T.land[:, 64:128, :], "llit")
 
+    mm, gr, gb = T.ci[:, 128:256], T.ci[:, 256:384], T.ci[0:8, 384:512]
     ms(T.lnf[:, 0:1], 0.0)
     ms(T.hf[:, 0:1], 0.0)
     ms(T.ones[:, :], 1.0)
-    ms(T.fl7[0:64, :], 0.0)
-    ms(C("ma0"), 0.0)
-    ms(C("ia0"), 0.0)
-    ms(C("zero"), 0.0)
-    my3 = ms(T.Y[:, Y3:Y3 + 2176], 0.0)
-    a1 = ts(T.pint[:, 1:2], T.pint[:, 0:1], 15, None, OP.bitwise_and, None, [kp])
-    a2 = ts(T.pint[:, 2:3], T.pint[:, 0:1], 5, None, OP.logical_shift_right)
+    for n in ("ma0", "ia0", "zero"):
+        ms(C(n), 0.0)
+    ts(T.pint[:, 1:2], T.pint[:, 0:1], 15, None, OP.bitwise_and, None, [kp])
+    ts(T.pint[:, 2:3], T.pint[:, 0:1], 5, None, OP.logical_shift_right)
     a3 = ts(T.pint[:, 3:4], T.pint[:, 0:1], 4, 1, OP.logical_shift_right, OP.bitwise_and)
-    c1 = tt(C("cd"), C("key"), C("ac"), OP.subtract, [k3])
-    c2 = ts(C("phl"), C("ac"), 16.0, None, OP.mult)
+    ts(mm, T.ci[:, 0:128], 15, None, OP.bitwise_and, None, [kc])
+    ts(gr, T.ci[:, 0:128], 4, None, OP.logical_shift_right)
+    gi = ts(gb, T.ci[0:8, 0:128], 5, None, OP.logical_shift_right)
     b1 = cp(T.pf[:, 0:4], T.pint[:, 0:4], [a3])
-    c3 = ts(C("phn"), C("cd"), 128.0, None, OP.mult, None, [c1])
-    g16 = ts(C("g16"), C("grp"), 16.0, None, OP.mult, None, [k4])
+    cp(C("cc"), T.ci[:, 0:128])
     ts(T.pf[:, 4:5], T.pf[:, 2:3], 2.0, None, OP.mult, None, [b1])
     ts(T.pf[:, 6:7], T.pf[:, 2:3], 2.0, 1.0, OP.mult, OP.add)
     ts(T.pf[:, 5:6], T.pf[:, 1:2], 16.0, None, OP.mult)
     ts(T.pf[:, 7:8], T.pf[:, 3:4], 0.0, None, OP.is_equal)
     ts(T.pf[:, 8:9], T.pf[:, 0:1], 32.0, 2176.0, OP.is_ge, OP.mult)
-    ts(T.pf[:, 9:10], T.pf[:, 3:4], 0.0, 2176.0, OP.is_equal, OP.mult)
+    ts(T.pf[:, 9:10], T.pf[:, 3:4], 0.0, 4352.0, OP.is_equal, OP.mult)
+    ts(T.pf[:, 11:12], T.pf[:, 0:1], -1.0, None, OP.add)
     b2 = ts(T.pf[:, 10:11], T.pf[:, 0:1], 16.0, 2432.0, OP.is_ge, OP.mult)
-    mm = tt(C("mm"), C("cc"), C("g16"), OP.subtract, [g16])
-    ident = ts(C("id"), C("dm"), 0.0, None, OP.is_equal, None, [k6])
-    ts(C("pln"), C("ac"), T.pf[:, 1:2], None, OP.add, None, [b2])
+    ts(C("id"), T.ci[:, 0:128], T.pf[:, 0:1], None, OP.is_equal)
+    c1 = tt(C("cd"), C("key"), C("ac"), OP.subtract, [kk])
+    ts(C("phl"), C("ac"), 16.0, None, OP.mult)
+    ts(C("ma"), gr, T.pf[:, 4:5], None, OP.is_equal, None, [b2])
+    mb = ts(C("mb"), gr, T.pf[:, 6:7], None, OP.is_equal)
+    ts(C("m1"), mm, 1.0, None, OP.add)
+    ts(C("m99"), mm, -99.0, None, OP.add)
+    ts(C("pln"), C("ac"), T.pf[:, 1:2], None, OP.add)
+    ts(C("phn"), C("cd"), 128.0, None, OP.mult, None, [c1])
     ts(C("pll"), C("cd"), T.pf[:, 5:6], None, OP.add)
-    ts(C("ma"), C("grp"), T.pf[:, 4:5], None, OP.is_equal)
-    mb = ts(C("mb"), C("grp"), T.pf[:, 6:7], None, OP.is_equal)
-    ts(C("m1"), C("mm"), 1.0, None, OP.add, None, [mm])
-    ts(C("m99"), C("mm"), -99.0, None, OP.add)
     tt(C("mall"), C("ma"), C("mb"), OP.add, [mb])
     cp(Cs("ma0", 128, 0, 16), Cs("ma", 128, 0, 16))
-    x = tt(C("ma1"), C("ma"), C("ma0"), OP.subtract, al("cv"))
+    cp(Cs("ia0", 128, 0, 16), Cs("id", 128, 0, 16))
     ts(C("ia"), C("id"), T.pf[:, 7:8], None, OP.mult)
     ts(C("ib"), C("id"), T.pf[:, 3:4], None, OP.mult)
-    cp(Cs("ia0", 128, 0, 16), Cs("id", 128, 0, 16))
-    cp(T.id16[0:16, :], Cs("id", 16, 0, 16))
-    x = tt(C("ir"), C("id"), C("ia0"), OP.subtract, al("cv"))
-    for n in ("all", "a0", "b", "a1"):
+    ts(Cs("sel0", 8, 0, 128), gb, 2.0, T.pf[0:8, 0:1], OP.mult, OP.is_equal)
+    ts(Cs("sel1", 8, 0, 128), gb, 2.0, T.pf[0:8, 11:12], OP.mult, OP.is_equal)
+    for r in (2, 4, 6):
+        x = ts(Cs("r%d" % r, 8, 0, 128), Cs("zero", 8, 0, 128), T.pf[0:8, 0:1], float(r), OP.add, OP.is_equal)
+    tt(C("ma1"), C("ma"), C("ma0"), OP.subtract, [x])
+    x = tt(C("ir"), C("id"), C("ia0"), OP.subtract)
+    for n in ("all", "a", "a0", "b"):
         x = tt(C("g" + n), C("m1"), C("m" + n), OP.mult)
-    for n in ("b", "a1"):
-        x = tt(C("s" + n), C("m99"), C("m" + n), OP.mult)
-    need("v", al("cv"))
-    for n in ("all", "a0", "b", "a1"):
+    tt(C("sb"), C("m99"), C("mb"), OP.mult)
+    tt(C("ga1"), C("m1"), C("ma1"), OP.mult, [x])
+    x = tt(C("sa1"), C("m99"), C("ma1"), OP.mult)
+    need("v", [x])
+    for n in ("all", "a", "a0", "b", "a1"):
         ts(C("G" + n), C("g" + n), -1.0, None, OP.add)
     for n in ("b", "a1"):
-        ts(C("L" + n), C("s" + n), 99.0, None, OP.add)
-    ts(Cs("sel0", 8, 0, 128), Cs("gb2", 8, 0, 128), T.pf[0:8, 0:1], None, OP.is_equal, None, [k5])
-    ts(Cs("sel1", 8, 0, 128), Cs("gb2", 8, 0, 128), 1.0, T.pf[0:8, 0:1], OP.add, OP.is_equal)
-    for r in (2, 4, 6):
-        setup = ts(Cs("r%d" % r, 8, 0, 128), Cs("zero", 8, 0, 128), T.pf[0:8, 0:1], float(r), OP.add, OP.is_equal)
+        setup = ts(C("L" + n), C("s" + n), 99.0, None, OP.add)
+    ms(T.u0[:, :], 0)
+    ms(T.fl7[0:64, :], 0.0)
+    my3 = ms(T.Y[:, Y3:Y3 + 2176], 0.0)
 
-    i1 = act(T.W[:, 512:1024], T.W[:, 0:512], [kid], bias=512.0)
-    i2 = act(T.W[:, 1024:2048], T.W[:, 0:1024], [i1], bias=1024.0)
+    x = act(T.W[:, 256:512], T.W[:, 0:256], [kid], bias=256.0)
+    x = act(T.W[:, 512:1024], T.W[:, 0:512], [x], bias=512.0)
+    i2 = act(T.W[:, 1024:2048], T.W[:, 0:1024], [x], bias=1024.0)
     for y in (Y3, Y7, Y11):
         act(T.Y[:, y + SYM:y + SYM + 256], T.W[:, 0:256])
 
-    P = {n: T["p%d" % n][:, 0:128] for n in (0, 1, 2, 3, 4)}
-    for n in (1, 2, 3):
+    P = {n: T["p%d" % n][:, 0:128] for n in (1, 2, 3, 4)}
+    for n in (1, 2):
         mms(P[n], [(C("id"), C("phn")), (C("id"), C("pln"))], True, False, [setup])
+    mms(P[3], [(C("ia"), C("phn")), (C("ia"), C("pln")), (C("ib"), C("phl")), (C("ib"), C("pll"))], True, False, [])
     mms(P[4], [(C("ia0"), C("phn")), (C("ia0"), C("pln")), (C("ir"), C("phl")), (C("ir"), C("pll"))], True, False, [])
-    mms(P[0], [(C("ib"), C("phl")), (C("ib"), C("pll"))], True, False, [])
 
     n1 = cp(T.lnf[0:16, 1:33], T.ln2[0:16, :], al("lfr"))
     n2 = tt(T.hf[0:16, 1:33], T.fr[0:16, :], T.ln2[0:16, :], OP.add)
     need("v", [n1])
     n3 = tok(g.vector.tensor_tensor_scan(T.first[0:16, :], T.lnf[0:16, 0:32], T.ones[0:16, :], 0.0, OP.add, OP.mult), "cv")
-    n4 = tt(T.dr[0:16, :], T.fr[0:16, :], T.hf[0:16, 0:32], OP.subtract, [n2])
+    n4 = tt(T.di[0:16, :], T.fr[0:16, :], T.hf[0:16, 0:32], OP.subtract, [n2])
+    n3 = cp(T.fi[0:16, :], T.first[0:16, :], [n3])
+
+    def Q(k):
+        return T.qi[0:16, 32 * k:32 * k + 32]
+    ts(Q(2), T.di[0:16, :], -64, None, OP.bitwise_and, None, [n4])
+    ts(Q(3), T.di[0:16, :], 63, None, OP.bitwise_and)
+    q0 = ts(Q(0), T.fi[0:16, :], 15, None, OP.bitwise_and, None, [n3])
+    q1 = ts(Q(1), T.fi[0:16, :], 4, None, OP.logical_shift_right)
+    x = cp(T.qb[0:16, 0:128], T.qi[0:16, 0:128], [q1])
+
+    def turn(dst, ks, toks):
+        need("p", toks)
+        for i, k in enumerate(ks):
+            for b in range(4):
+                ins = g.tensor.matmul(dst[32 * b:32 * b + 32, 4 * i:4 * i + 4], T.qb[0:16, 32 * k:32 * k + 32],
+                                      Cs("id", 16, 4 * b, 4 * b + 4), True, True)
+        return tok(ins, "cp")
+    zz = turn(T.px[:, 0:16], (1, 2, 3, 0), [x])
     nl = cp(Cs("lit", 8, 0, 128), T.litr[0:8, :], al("llit"))
-    for q, (buf, t) in enumerate(((T.first, n3), (T.dr, n4))):
-        need("p", [t])
-        for b in range(4):
-            ins = g.tensor.matmul(T.px[32 * b:32 * b + 32, 4 * q:4 * q + 4], buf[0:16, 0:32], T.id16[0:16, 4 * b:4 * b + 4], True, True)
-    tx = tok(ins, "cp")
     need("p", [nl])
     for k, n in enumerate(("sel0", "sel1", "r2", "r4")):
         ins = g.tensor.matmul(T.pta[:, 128 * k:128 * k + 128], Cs(n, 8, 0, 128), Cs("lit", 8, 0, 128), True, True)
     tta = tok(ins, "cp")
-    ttb = tok(g.tensor.matmul(T.ptb[:, 0:128], Cs("r6", 8, 0, 128), Cs("lit", 8, 0, 128), True, True), "cp")
+    g.tensor.matmul(T.ptb[:, 0:128], Cs("r6", 8, 0, 128), Cs("lit", 8, 0, 128), True, True)
     code = T.pf[:, 8:9]
     act(T.W[:, ID + 2048:ID + 2176], T.pta[:, 0:128], [tta, b2], bias=code)
     act(T.W[:, S1 + 2048:S1 + 2176], T.pta[:, 0:128], bias=code)
     act(T.W[:, S2 + 2048:S2 + 2176], T.pta[:, 128:256], bias=code)
     tails = act(T.W[:, S3 + 2048:S3 + 2176], T.pta[:, 128:256], bias=code)
 
-    x = cp(T.xi[:, :], T.px[:, 0:8], [tx])
-    ts(T.zi[:, 0:4], T.xi[:, 0:4], 15, None, OP.bitwise_and, None, [x])
-    zh = ts(T.zi[:, 4:8], T.xi[:, 0:4], 4, None, OP.logical_shift_right)
-    ts(T.zi[:, 8:12], T.xi[:, 4:8], -64, None, OP.bitwise_and)
-    x = ts(T.zi[:, 12:16], T.xi[:, 4:8], 63, None, OP.bitwise_and)
-    zz = cp(T.zf[:, 0:16], T.zi[:, 0:16], [x])
+    def X(k, t):
+        return T.px[:, 4 * k + t:4 * k + t + 1]
 
     def Z(k, t):
         return T.zf[:, 4 * k + t:4 * k + t + 1]
 
     def nat(n, t, m, toks, stop):
         need("v", toks)
-        w = "%d%s" % (t, n)
+        w = "%d%s" % (t, m)
         for h in (0, 1):
-            ts(C("n1" + w + str(h)), C("cc"), Z(1, t), Z(2 + h, t), OP.is_gt, OP.mult)
+            ts(C("n1" + w + str(h)), C("cc"), X(0, t), X(1 + h, t), OP.is_gt, OP.mult)
         for h in (0, 1):
-            ts(C("n2" + w + str(h)), C("cc"), Z(1, t), Z(2 + h, t), OP.is_equal, OP.mult)
-        x = ts(C("nl" + w), C("G" + m), Z(0, t), None, OP.is_ge)
+            ts(C("n2" + w + str(h)), C("cc"), X(0, t), X(1 + h, t), OP.is_equal, OP.mult)
+        x = ts(C("nl" + w), C("G" + m), X(3, t), None, OP.is_ge)
         return mms(P[n], [(C("m" + m), C("n1" + w + str(h))) for h in (0, 1)] +
                    [(C("nl" + w), C("n2" + w + str(h))) for h in (0, 1)], False, stop, [x])
 
     def lst(n, t, m, toks, stop):
         need("v", toks)
-        w = "%d%s" % (t, n)
+        w = "%d%s" % (t, m)
         pr = []
-        for k, (row, z, op, side, lop) in enumerate((("ac", 5, OP.is_gt, "L", OP.is_lt), ("ac", 5, OP.is_ge, "G", OP.is_gt),
-                                                     ("key", 6, OP.is_ge, "G", OP.is_equal))):
+        for k, (row, z, op, side, lop) in enumerate((("ac", 1, OP.is_gt, "L", OP.is_lt), ("ac", 1, OP.is_ge, "G", OP.is_gt),
+                                                     ("key", 2, OP.is_ge, "G", OP.is_equal))):
             for h in (0, 1):
-                ts(C("q%d%s%d" % (k, w, h)), C(row), Z(z, t), Z(2 + h, t), op, OP.mult)
-            x = ts(C("ql%d%s" % (k, w)), C(side + m), Z(4, t), None, lop)
+                ts(C("q%d%s%d" % (k, w, h)), C(row), Z(z, t), X(1 + h, t), op, OP.mult)
+            x = ts(C("ql%d%s" % (k, w)), C(side + m), Z(0, t), None, lop)
             pr += [(C("ql%d%s" % (k, w)), C("q%d%s%d" % (k, w, h))) for h in (0, 1)]
         return mms(P[n], pr, False, stop, [x])
 
-    def gather(out, o0, win, w0, w1, lu, nv, toks, pre=()):
+    def gather(out, o0, win, w0, w1, lu, nv, toks):
         need("v", toks)
         tv = tok(g.vector.tensor_copy(out[:, o0:o0 + 16 * nv], win[:, w0:w1].indirect(lu[:, 0:nv])), "cv")
         need("a", toks)
@@ -290,60 +303,60 @@ def rank_program(g, core, T, topo):
             g.remote_dma_fused(trs, local_sem=T.sem.rloc)
 
     t1 = nat(1, 0, "all", [zz, setup], True)
+    ts(Q(4), Q(1), 15, None, OP.bitwise_and)
+    x = ts(Q(5), T.fi[0:16, :], 4, 112, OP.logical_shift_right, OP.bitwise_and)
+    x = tt(Q(6), Q(5), Q(0), OP.add, [x])
+    x = cp(T.qb[0:16, 128:224], T.qi[0:16, 128:224], [x])
+    tz = turn(T.ptb[:, 128:140], (4, 5, 6), [x])
     e1 = cp(T.u1[:, :], T.p1[:, 0:128], [t1])
     t2 = nat(2, 1, "all", [], True)
-    s1 = gather(T.W, S1, T.W, ID, ID + 2176, T.u1, 52, [e1, i2, tails])
+    zl = cp(T.zf[:, 0:12], T.ptb[:, 128:140], [tz])
+    nat(4, 3, "a0", [], False)
+    s1 = gather(T.W, S1, T.W, ID, ID + 2176, T.u1, NV[0], [e1, i2, tails])
     e2 = cp(T.u2[:, :], T.p2[:, 0:128], [t2])
     elr = act(T.lr[:, :], T.p1[:, 0:128], [e1])
     dma("s", T.fl0[0:16, :], T.lr[32:48, :], "dl0", [elr])
     dma("s", T.fl6[16:32, :], T.lr[64:80, :], "dl6")
     dma("s", T.fl7[64:80, :], T.lr[96:112, :], "dl7")
     ship(0, T.W[0:1, S1:S1 + 2048], "sh0", s1)
-    t3 = nat(3, 2, "all", [], True)
-    ts(T.zi[:, 16:20], T.zi[:, 4:8], 15, None, OP.bitwise_and, None, [zh])
-    x = ts(T.zi[:, 20:24], T.zi[:, 4:8], 112, None, OP.bitwise_and)
-    x = cp(T.zf[:, 16:24], T.zi[:, 16:24], [x])
-    zl = tt(T.zf[:, 24:28], T.zf[:, 20:24], T.zf[:, 0:4], OP.add, [x])
-    s2 = gather(T.W, S2, T.W, S1, S1 + 2176, T.u2, 50, s1 + [e2])
+    nat(3, 2, "a", [zl], False)
+    t3 = lst(3, 2, "b", [], True)
+    s2 = gather(T.W, S2, T.W, S1, S1 + 2176, T.u2, NV[1], s1 + [e2])
     e3 = cp(T.u3[:, :], T.p3[:, 0:128], [t3])
     ship(1, T.W[0:1, S2:S2 + 2048], "sh0", s2)
     act(T.W[:, S4 + 2048:S4 + 2176], T.pta[:, 256:384])
-    nat(4, 3, "a0", [zl], False)
     lst(4, 3, "a1", [], False)
-    s3 = gather(T.W, S3, T.W, S2, S2 + 2176, T.u3, 46, s2 + [e3])
+    t4 = lst(4, 1, "b", [], True)
+    s3 = gather(T.W, S3, T.W, S2, S2 + 2176, T.u3, NV[2], s2 + [e3])
     act(T.Y[:, Y7 + 2048:Y7 + 2176], T.pta[:, 384:512])
-    t4 = lst(4, 2, "b", [], True)
     e4 = ts(T.u4[:, :], T.p4[:, 0:128], T.pf[:, 9:10], None, OP.add, None, [t4])
+    dma("s", T.fl5[0:16, :], T.W[48:49, S3:S3 + 2048], "dl5", s3)
+    dma("s", T.fl6[48:64, :], T.W[80:81, S3:S3 + 2048], "dl6")
+    dma("s", T.fl7[96:112, :], T.W[112:113, S3:S3 + 2048], "dl7", [setup])
     ship(2, T.W[0:1, S3:S3 + 2048], "sh0", s3)
-    s4 = gather(T.W, S4, T.W, S2, S3 + 2176, T.u4, 60, s3 + [e4])
-    rows = T.W
-    dma("s", T.Y[0:128:16, Y3:Y3 + 2048], rows[0:8, S4:S4 + 2048], "dy3", s4 + [my3])
-    dma("a", T.fl5[16:128, :], rows[32:39, S4:S4 + 2048], "dl5", s4)
-    dma("s", T.fl5[0:16, :], rows[48:49, S4:S4 + 2048], "dl5")
-    dma("s", T.fl6[64:128, :], rows[64:68, S4:S4 + 2048], "dl6")
-    dma("s", T.fl6[48:64, :], rows[80:81, S4:S4 + 2048], "dl6")
-    dma("s", T.fl7[96:112, :], rows[112:113, S4:S4 + 2048], "dl7", [setup])
-    dma("s", T.fl7[112:128, :], rows[96:97, S4:S4 + 2048], "dl7")
+    s4 = gather(T.W, S4, T.W, S1, S3 + 2176, T.u4, NV[3], s3 + [e4])
+    dma("s", T.Y[0:128:16, Y3:Y3 + 2048], T.W[0:8, S4:S4 + 2048], "dy3", s4 + [my3])
+    dma("a", T.fl5[16:128, :], T.W[32:39, S4:S4 + 2048], "dl5", s4)
+    dma("s", T.fl6[64:128, :], T.W[64:68, S4:S4 + 2048], "dl6")
+    dma("s", T.fl6[0:16, :], T.W[48:49, S4:S4 + 2048], "dl6")
+    dma("s", T.fl6[32:48, :], T.W[80:81, S4:S4 + 2048], "dl6")
+    dma("s", T.fl7[80:96, :], T.W[112:113, S4:S4 + 2048], "dl7")
+    dma("s", T.fl7[112:128, :], T.W[96:97, S4:S4 + 2048], "dl7")
     ship(3, T.W[0:1, S4:S4 + 2048], "sh0", s4)
-    t0 = lst(0, 1, "b", [], True)
-    x = cp(T.u0[:, :], T.p0[:, 0:128], [t0])
-    e0 = ts(T.u0[0:16, :], T.fl0[0:16, :], float(S4 - S1), None, OP.add, None, al("dl0") + [x])
-    s0 = gather(T.O, 0, T.W, S1, S4 + 2176, T.u0, 54, s4 + [e0])
-    act(T.Y[:, Y11 + 2048:Y11 + 2176], T.ptb[:, 0:128], [ttb])
-    dma("s", T.fl6[0:16, :], T.O[48:49, :], "dl6", s0)
-    dma("s", T.fl6[32:48, :], T.O[80:81, :], "dl6")
-    dma("s", T.fl7[80:96, :], T.O[112:113, :], "dl7")
+    e0 = cp(T.u0[0:16, :], T.fl0[0:16, :], al("dl0") + [my3])
+    s0 = gather(T.O, 0, T.W, S4, S4 + 2176, T.u0, NV[4], s4 + [e0])
+    act(T.Y[:, Y11 + 2048:Y11 + 2176], T.ptb[:, 0:128], [tz, zl])
     ship(4, T.O[0:1, :], "sh2", s0)
     e5 = cp(T.u5[:, :], T.fl5[:, :], al("dl5"))
-    s5 = gather(T.Y, Y7, T.Y, Y3, Y3 + 2432, T.u5, 64, al("dy3") + [e5])
-    ship2(3, T.Y[0:32:16, Y7:Y7 + 2048], "sh1", s5)
+    s5 = gather(T.Y, Y7, T.Y, Y3, Y3 + 2432, T.u5, NV[5], al("dy3") + [e5])
     e6 = ts(T.u6[:, :], T.fl6[:, :], T.pf[:, 10:11], None, OP.add, None, al("dl6"))
-    s6 = gather(T.Y, Y11, T.Y, Y3, Y7 + 2432, T.u6, 64, s5 + [e6])
+    ship2(3, T.Y[0:32:16, Y7:Y7 + 2048], "sh1", s5)
+    s6 = gather(T.Y, Y11, T.Y, Y3, Y7 + 2432, T.u6, NV[6], s5 + [e6])
+    e7 = cp(T.u7[:, :], T.fl7[:, :], al("dl7"))
     ship2(4, T.Y[16:48:16, Y11:Y11 + 2048], "sh2", s6)
     ship2(5, T.Y[48:80:16, Y11:Y11 + 2048], "sh2", s6)
     ship(5, T.Y[0:1, Y11:Y11 + 2048], "sh2", s6)
-    e7 = cp(T.u7[:, :], T.fl7[:, :], al("dl7"))
-    s7 = gather(T.Y, YF, T.Y, Y11, Y11 + 2432, T.u7, 64, s6 + [e7])
+    s7 = gather(T.Y, YF, T.Y, Y11, Y11 + 2432, T.u7, NV[7], s6 + [e7])
     ship2(6, T.Y[64:96:16, YF:YF + 2048], "sh3", s7)
     ship2(7, T.Y[96:128:16, YF:YF + 2048], "sh3", s7, "a")
     for c in range(4):

@@ -2,9 +2,9 @@ from concourse.bass import DstId, RemoteDMATransfer
 from concourse.mybir import AluOpType as OP, ActivationFunctionType as AF
 
 ID, S1, S2, S3, S4, WEND = 0, 2176, 4352, 6528, 8704, 10880
-Y3, Y7, Y11, YF, YEND = 0, 2432, 4864, 7296, 9344
+Y7, Y3, Y11, YF, YEND = 0, 2432, 4864, 7296, 9344
 SYM = 2176
-NV = [44, 42, 42, 62, 64, 64, 64, 64]
+NV = [40, 42, 42, 64, 64, 64, 64, 64]
 SCRATCH = {
     "stage": ("dram", [8, 128, 2], "int32"), "land": ("dram", [8, 128, 2], "int32"),
     "ost": ("dram", [8, 128, 32], "float32"), "yland": ("dram", [8, 128, 32], "float32"),
@@ -14,18 +14,18 @@ SCRATCH = {
     "fi": ("sbuf", [128, 32], "int32"), "di": ("sbuf", [128, 32], "int32"),
     "qi": ("sbuf", [128, 224], "int32"), "qb": ("sbuf", [128, 224], "bfloat16"),
     "pint": ("sbuf", [128, 8], "int32"), "pf": ("sbuf", [128, 16], "float32"), "zf": ("sbuf", [128, 16], "float32"),
-    "ci": ("sbuf", [128, 512], "int32"), "cb": ("sbuf", [128, 128 * 96], "bfloat16"),
+    "cb": ("sbuf", [128, 128 * 96], "bfloat16"),
     "W": ("sbuf", [128, WEND], "float32"), "Y": ("sbuf", [128, YEND], "float32"), "O": ("sbuf", [128, 2048], "float32"),
-    "lr": ("sbuf", [128, 128], "float32"),
+    "litx": ("sbuf", [128, 128], "int32"), "litf": ("sbuf", [128, 128], "float32"),
 }
-for _n in ("l0", "l5", "l6", "l7"):
+for _n in ("l5", "l6", "l7"):
     SCRATCH["f" + _n] = ("sbuf", [128, 128], "float32")
 for _n in ("1", "2", "3", "4", "0", "5", "6", "7"):
     SCRATCH["u" + _n] = ("sbuf", [128, 128], "uint16")
 for _n in ("p1", "p2", "p3", "p4", "px", "pta", "ptb"):
     SCRATCH[_n] = ("psum", [128, 512], "float32")
-SEMAPHORES = ["cv", "ca", "cp", "cg", "ld", "own", "arr", "lfr", "llit", "dl0", "dy3", "dl5", "dl6", "dl7",
-              "sh0", "sh1", "sh2", "sh3", "shown", "rloc", "yarr", "yst"]
+SEMAPHORES = ["cv", "ca", "cp", "cg", "ld", "own", "arr", "lfr", "llit", "llx", "dl0", "du6", "du7", "dy3", "dl5", "dl6",
+              "dl7", "sh0", "sh1", "sh2", "sh3", "shown", "rloc", "yarr", "yst"]
 CALLS = [[0, 1], [3], [2, 4, 5], [6, 7]]
 
 
@@ -111,11 +111,13 @@ def rank_program(g, core, T, topo):
     dma("a", T.land[me:me + 1, 0:32, :], T.frm[me:me + 1, :], "own")
     dma("s", T.land[me:me + 1, 32:64, :], T.ln[me:me + 1, :], "own")
     dma("a", T.land[me:me + 1, 64:128, :], T.lit[me:me + 1, :], "own")
+    for n in ("Gall", "Ga", "Gb", "Ga1", "Lb", "La1", "sa0", "sa9"):
+        C(n)
     kp = iota(T.pint[:, 0:1], [[0, 1]], 0, 1)
-    kc = iota(T.ci[:, 0:128], [[1, 128]], 0, 0)
-    ka = iota(C("ac"), [[0, 16], [16, 8]], 0, 0)
-    kk = iota(C("key"), [[1, 16], [16, 8]], 0, 0)
-    kid = iota(T.W[:, 0:256], [[1, 256]], 0, 0)
+    iota(C("tm"), [[0, 4], [100, 2], [1, 16]], 0, 0)
+    iota(C("tb"), [[2, 4], [0, 32]], 0, 0)
+    kt = iota(C("tab"), [[2, 4], [100, 2], [0, 16]], 0, 0)
+    kcc = iota(C("cc"), [[1, 128]], 0, 0)
     need("g", al("ld"))
     trs = []
     for r in range(8):
@@ -133,62 +135,54 @@ def rank_program(g, core, T, topo):
     dma("s", T.fr[0:16, :], T.land[:, 0:32, :], "lfr")
     dma("s", T.litr[0:8, :], T.land[:, 64:128, :], "llit")
 
-    mm, gr, gb = T.ci[:, 128:256], T.ci[:, 256:384], T.ci[0:8, 384:512]
+    kid = iota(T.W[:, 0:256], [[1, 256]], 0, 0)
+    iota(Cs("n16", 16, 0, 128), [[16, 128]], 0, 0)
+    iota(Cs("nk", 16, 0, 128), [[0, 128]], 0, 1)
+    iota(Cs("l256", 16, 0, 128), [[0, 16], [256, 8]], 0, 0)
+    kpl = iota(Cs("l16", 16, 0, 128), [[1, 16], [0, 8]], 0, 16)
+    iota(C("ac"), [[0, 16], [16, 8]], 0, 0)
+    kk = iota(C("key"), [[1, 16], [16, 8]], 0, 0)
+    my3 = iota(T.Y[:, Y3:Y3 + 2176], [[0, 2176]], 0, 0)
     ms(T.lnf[:, 0:1], 0.0)
     ms(T.hf[:, 0:1], 0.0)
     ms(T.ones[:, :], 1.0)
-    for n in ("ma0", "ia0", "zero"):
-        ms(C(n), 0.0)
-    ts(T.pint[:, 1:2], T.pint[:, 0:1], 15, None, OP.bitwise_and, None, [kp])
-    ts(T.pint[:, 2:3], T.pint[:, 0:1], 5, None, OP.logical_shift_right)
-    a3 = ts(T.pint[:, 3:4], T.pint[:, 0:1], 4, 1, OP.logical_shift_right, OP.bitwise_and)
-    ts(mm, T.ci[:, 0:128], 15, None, OP.bitwise_and, None, [kc])
-    ts(gr, T.ci[:, 0:128], 4, None, OP.logical_shift_right)
-    gi = ts(gb, T.ci[0:8, 0:128], 5, None, OP.logical_shift_right)
-    b1 = cp(T.pf[:, 0:4], T.pint[:, 0:4], [a3])
-    cp(C("cc"), T.ci[:, 0:128])
-    ts(T.pf[:, 4:5], T.pf[:, 2:3], 2.0, None, OP.mult, None, [b1])
-    ts(T.pf[:, 6:7], T.pf[:, 2:3], 2.0, 1.0, OP.mult, OP.add)
-    ts(T.pf[:, 5:6], T.pf[:, 1:2], 16.0, None, OP.mult)
-    ts(T.pf[:, 7:8], T.pf[:, 3:4], 0.0, None, OP.is_equal)
-    ts(T.pf[:, 8:9], T.pf[:, 0:1], 32.0, 2176.0, OP.is_ge, OP.mult)
-    ts(T.pf[:, 9:10], T.pf[:, 3:4], 0.0, 4352.0, OP.is_equal, OP.mult)
-    ts(T.pf[:, 11:12], T.pf[:, 0:1], -1.0, None, OP.add)
-    b2 = ts(T.pf[:, 10:11], T.pf[:, 0:1], 16.0, 2432.0, OP.is_ge, OP.mult)
-    ts(C("id"), T.ci[:, 0:128], T.pf[:, 0:1], None, OP.is_equal)
-    c1 = tt(C("cd"), C("key"), C("ac"), OP.subtract, [kk])
-    ts(C("phl"), C("ac"), 16.0, None, OP.mult)
-    ts(C("ma"), gr, T.pf[:, 4:5], None, OP.is_equal, None, [b2])
-    mb = ts(C("mb"), gr, T.pf[:, 6:7], None, OP.is_equal)
-    ts(C("m1"), mm, 1.0, None, OP.add)
-    ts(C("m99"), mm, -99.0, None, OP.add)
-    ts(C("pln"), C("ac"), T.pf[:, 1:2], None, OP.add)
-    ts(C("phn"), C("cd"), 128.0, None, OP.mult, None, [c1])
-    ts(C("pll"), C("cd"), T.pf[:, 5:6], None, OP.add)
-    tt(C("mall"), C("ma"), C("mb"), OP.add, [mb])
-    cp(Cs("ma0", 128, 0, 16), Cs("ma", 128, 0, 16))
-    cp(Cs("ia0", 128, 0, 16), Cs("id", 128, 0, 16))
-    ts(C("ia"), C("id"), T.pf[:, 7:8], None, OP.mult)
-    ts(C("ib"), C("id"), T.pf[:, 3:4], None, OP.mult)
-    ts(Cs("sel0", 8, 0, 128), gb, 2.0, T.pf[0:8, 0:1], OP.mult, OP.is_equal)
-    ts(Cs("sel1", 8, 0, 128), gb, 2.0, T.pf[0:8, 11:12], OP.mult, OP.is_equal)
-    for r in (2, 4, 6):
-        x = ts(Cs("r%d" % r, 8, 0, 128), Cs("zero", 8, 0, 128), T.pf[0:8, 0:1], float(r), OP.add, OP.is_equal)
-    tt(C("ma1"), C("ma"), C("ma0"), OP.subtract, [x])
-    x = tt(C("ir"), C("id"), C("ia0"), OP.subtract)
-    for n in ("all", "a", "a0", "b"):
-        x = tt(C("g" + n), C("m1"), C("m" + n), OP.mult)
-    tt(C("sb"), C("m99"), C("mb"), OP.mult)
-    tt(C("ga1"), C("m1"), C("ma1"), OP.mult, [x])
-    x = tt(C("sa1"), C("m99"), C("ma1"), OP.mult)
-    need("v", [x])
-    for n in ("all", "a", "a0", "b", "a1"):
-        ts(C("G" + n), C("g" + n), -1.0, None, OP.add)
-    for n in ("b", "a1"):
-        setup = ts(C("L" + n), C("s" + n), 99.0, None, OP.add)
+    ms(T.cb[:, 0:512], -1.0)
+    ms(T.cb[:, 512:768], 99.0)
+    ms(T.cb[:, 768:1024], 0.0)
+    mlx = ms(T.litx[0:128, :], 0)
     ms(T.u0[:, :], 0)
-    ms(T.fl7[0:64, :], 0.0)
-    my3 = ms(T.Y[:, Y3:Y3 + 2176], 0.0)
+    fill = ms(T.u7[:, :], 0)
+    p0, p2b, off4, code, off6 = [T.pf[:, i:i + 1] for i in range(5)]
+    ts(T.pint[:, 1:2], T.pint[:, 0:1], 5, None, OP.logical_shift_right, None, [kp])
+    x = ts(T.pint[:, 2:3], T.pint[:, 0:1], 4, 1, OP.logical_shift_right, OP.bitwise_and)
+    cp(p0, T.pint[:, 0:1])
+    ts(p2b, T.pint[:, 1:2], 2.0, None, OP.mult, None, [x])
+    ts(off4, T.pint[:, 2:3], 0.0, 4352.0, OP.is_equal, OP.mult)
+    ts(code, T.pint[:, 0:1], 32.0, 2176.0, OP.is_ge, OP.mult)
+    b2 = ts(off6, T.pint[:, 0:1], 16.0, 2432.0, OP.is_lt, OP.mult)
+    ts(Cs("selA", 16, 0, 128), Cs("tm", 16, 0, 128), T.pf[0:16, 0:1], None, OP.is_equal, None, [b2, kt])
+    x = ts(Cs("selB", 16, 0, 128), Cs("tm", 16, 0, 128), -100.0, T.pf[0:16, 0:1], OP.add, OP.is_equal)
+    ts(Cs("sel0", 8, 0, 128), Cs("tb", 8, 0, 128), T.pf[0:8, 0:1], None, OP.is_equal)
+    ts(Cs("sel1", 8, 0, 128), Cs("tb", 8, 0, 128), 1.0, T.pf[0:8, 0:1], OP.add, OP.is_equal)
+    ts(C("mall"), C("tb"), p2b, None, OP.is_equal)
+    ts(C("ma"), C("tab"), p2b, None, OP.is_equal)
+    need("v", [x])
+    cp(Cs("sa0", 16, 0, 16), Cs("selA", 16, 0, 16))
+    setup = cp(Cs("sa9", 16, 16, 128), Cs("selA", 16, 16, 128))
+
+    def block(n, b, c0):
+        k = 128 * slots[n] + 32 * b + c0
+        t = 128 * slots["tm"]
+        out, src = T.cb[32 * b:32 * b + 32, k:k + 16], T.cb[32 * b:32 * b + 32, t:t + 16]
+        if n == "Ga1" and b == 0:
+            return ts(out, src, 0.5, None, OP.add)
+        return cp(out, src)
+    for n, c0 in (("Gall", 0), ("Gall", 16), ("Ga", 0), ("Gb", 16), ("Lb", 16), ("Ga1", 0), ("La1", 0)):
+        for b in range(4):
+            gdone = block(n, b, c0)
+    x = cp(C("ac3"), C("ac"), [kk])
+    need("v", [x])
+    cp(Cs("ac3", 32, 0, 128), Cs("cc", 32, 0, 128), [kcc])
 
     x = act(T.W[:, 256:512], T.W[:, 0:256], [kid], bias=256.0)
     x = act(T.W[:, 512:1024], T.W[:, 0:512], [x], bias=512.0)
@@ -197,10 +191,16 @@ def rank_program(g, core, T, topo):
         act(T.Y[:, y + SYM:y + SYM + 256], T.W[:, 0:256])
 
     P = {n: T["p%d" % n][:, 0:128] for n in (1, 2, 3, 4)}
-    for n in (1, 2):
-        mms(P[n], [(C("id"), C("phn")), (C("id"), C("pln"))], True, False, [setup])
-    mms(P[3], [(C("ia"), C("phn")), (C("ia"), C("pln")), (C("ib"), C("phl")), (C("ib"), C("pll"))], True, False, [])
-    mms(P[4], [(C("ia0"), C("phn")), (C("ia0"), C("pln")), (C("ir"), C("phl")), (C("ir"), C("pll"))], True, False, [])
+
+    def place(n, nats, lists):
+        mms(P[n], [(Cs(w, 16, 0, 128), Cs(q, 16, 0, 128)) for w in nats for q in ("n16", "nk")] +
+            [(Cs(w, 16, 0, 128), Cs(q, 16, 0, 128)) for w in lists for q in ("l256", "l16")], True, False, [setup, kpl])
+    place(1, ("selA", "selB"), ())
+    place(2, ("selA", "selB"), ())
+    place(3, ("selA",), ("selB",))
+    place(4, ("sa0",), ("sa9", "selB"))
+
+    dma("s", T.litx[32:128:32, :], T.land[2:8:2, 64:128, :], "llx", [mlx])
 
     n1 = cp(T.lnf[0:16, 1:33], T.ln2[0:16, :], al("lfr"))
     n2 = tt(T.hf[0:16, 1:33], T.fr[0:16, :], T.ln2[0:16, :], OP.add)
@@ -213,7 +213,7 @@ def rank_program(g, core, T, topo):
         return T.qi[0:16, 32 * k:32 * k + 32]
     ts(Q(2), T.di[0:16, :], -64, None, OP.bitwise_and, None, [n4])
     ts(Q(3), T.di[0:16, :], 63, None, OP.bitwise_and)
-    q0 = ts(Q(0), T.fi[0:16, :], 15, None, OP.bitwise_and, None, [n3])
+    ts(Q(0), T.fi[0:16, :], 15, None, OP.bitwise_and, None, [n3])
     q1 = ts(Q(1), T.fi[0:16, :], 4, None, OP.logical_shift_right)
     x = cp(T.qb[0:16, 0:128], T.qi[0:16, 0:128], [q1])
 
@@ -222,16 +222,14 @@ def rank_program(g, core, T, topo):
         for i, k in enumerate(ks):
             for b in range(4):
                 ins = g.tensor.matmul(dst[32 * b:32 * b + 32, 4 * i:4 * i + 4], T.qb[0:16, 32 * k:32 * k + 32],
-                                      Cs("id", 16, 4 * b, 4 * b + 4), True, True)
+                                      Cs("selA", 16, 4 * b, 4 * b + 4), True, True)
         return tok(ins, "cp")
     zz = turn(T.px[:, 0:16], (1, 2, 3, 0), [x])
     nl = cp(Cs("lit", 8, 0, 128), T.litr[0:8, :], al("llit"))
     need("p", [nl])
-    for k, n in enumerate(("sel0", "sel1", "r2", "r4")):
+    for k, n in enumerate(("sel0", "sel1")):
         ins = g.tensor.matmul(T.pta[:, 128 * k:128 * k + 128], Cs(n, 8, 0, 128), Cs("lit", 8, 0, 128), True, True)
     tta = tok(ins, "cp")
-    g.tensor.matmul(T.ptb[:, 0:128], Cs("r6", 8, 0, 128), Cs("lit", 8, 0, 128), True, True)
-    code = T.pf[:, 8:9]
     act(T.W[:, ID + 2048:ID + 2176], T.pta[:, 0:128], [tta, b2], bias=code)
     act(T.W[:, S1 + 2048:S1 + 2176], T.pta[:, 0:128], bias=code)
     act(T.W[:, S2 + 2048:S2 + 2176], T.pta[:, 128:256], bias=code)
@@ -247,24 +245,24 @@ def rank_program(g, core, T, topo):
         need("v", toks)
         w = "%d%s" % (t, m)
         for h in (0, 1):
-            ts(C("n1" + w + str(h)), C("cc"), X(0, t), X(1 + h, t), OP.is_gt, OP.mult)
+            x = ts(C("n1" + w + str(h)), C("cc"), X(0, t), X(1 + h, t), OP.is_gt, OP.mult)
+            mms(P[n], [(C("m" + m), C("n1" + w + str(h)))], False, False, [x])
+        ts(C("nl" + w), C("G" + m), X(3, t), None, OP.is_ge)
         for h in (0, 1):
-            ts(C("n2" + w + str(h)), C("cc"), X(0, t), X(1 + h, t), OP.is_equal, OP.mult)
-        x = ts(C("nl" + w), C("G" + m), X(3, t), None, OP.is_ge)
-        return mms(P[n], [(C("m" + m), C("n1" + w + str(h))) for h in (0, 1)] +
-                   [(C("nl" + w), C("n2" + w + str(h))) for h in (0, 1)], False, stop, [x])
+            x = ts(C("n2" + w + str(h)), C("cc"), X(0, t), X(1 + h, t), OP.is_equal, OP.mult)
+            y = mms(P[n], [(C("nl" + w), C("n2" + w + str(h)))], False, stop and h == 1, [x])
+        return y
 
-    def lst(n, t, m, toks, stop):
+    def lst(n, t, m, row, toks, stop):
         need("v", toks)
         w = "%d%s" % (t, m)
-        pr = []
-        for k, (row, z, op, side, lop) in enumerate((("ac", 1, OP.is_gt, "L", OP.is_lt), ("ac", 1, OP.is_ge, "G", OP.is_gt),
-                                                     ("key", 2, OP.is_ge, "G", OP.is_equal))):
+        for k, (r, z, op, side, lop) in enumerate(((row, 1, OP.is_gt, "L", OP.is_lt), (row, 1, OP.is_ge, "G", OP.is_gt),
+                                                   ("key", 2, OP.is_ge, "G", OP.is_equal))):
+            ts(C("ql%d%s" % (k, w)), C(side + m), Z(0, t), None, lop)
             for h in (0, 1):
-                ts(C("q%d%s%d" % (k, w, h)), C(row), Z(z, t), X(1 + h, t), op, OP.mult)
-            x = ts(C("ql%d%s" % (k, w)), C(side + m), Z(0, t), None, lop)
-            pr += [(C("ql%d%s" % (k, w)), C("q%d%s%d" % (k, w, h))) for h in (0, 1)]
-        return mms(P[n], pr, False, stop, [x])
+                x = ts(C("q%d%s%d" % (k, w, h)), C(r), Z(z, t), X(1 + h, t), op, OP.mult)
+                y = mms(P[n], [(C("ql%d%s" % (k, w)), C("q%d%s%d" % (k, w, h)))], False, stop and k == 2 and h == 1, [x])
+        return y
 
     def gather(out, o0, win, w0, w1, lu, nv, toks):
         need("v", toks)
@@ -302,63 +300,65 @@ def rank_program(g, core, T, topo):
             need("g", al("sh%d" % c))
             g.remote_dma_fused(trs, local_sem=T.sem.rloc)
 
-    t1 = nat(1, 0, "all", [zz, setup], True)
+    t1 = nat(1, 0, "all", [zz, gdone], True)
     ts(Q(4), Q(1), 15, None, OP.bitwise_and)
     x = ts(Q(5), T.fi[0:16, :], 4, 112, OP.logical_shift_right, OP.bitwise_and)
     x = tt(Q(6), Q(5), Q(0), OP.add, [x])
-    x = cp(T.qb[0:16, 128:224], T.qi[0:16, 128:224], [x])
-    tz = turn(T.ptb[:, 128:140], (4, 5, 6), [x])
     e1 = cp(T.u1[:, :], T.p1[:, 0:128], [t1])
+    x = cp(T.qb[0:16, 128:224], T.qi[0:16, 128:224], [x])
     t2 = nat(2, 1, "all", [], True)
-    zl = cp(T.zf[:, 0:12], T.ptb[:, 128:140], [tz])
-    nat(4, 3, "a0", [], False)
+    tz = turn(T.ptb[:, 128:140], (4, 5, 6), [x])
     s1 = gather(T.W, S1, T.W, ID, ID + 2176, T.u1, NV[0], [e1, i2, tails])
     e2 = cp(T.u2[:, :], T.p2[:, 0:128], [t2])
-    elr = act(T.lr[:, :], T.p1[:, 0:128], [e1])
-    dma("s", T.fl0[0:16, :], T.lr[32:48, :], "dl0", [elr])
-    dma("s", T.fl6[16:32, :], T.lr[64:80, :], "dl6")
-    dma("s", T.fl7[64:80, :], T.lr[96:112, :], "dl7")
+    xl = cp(T.litf[:, :], T.litx[:, :], al("llx"))
+    need("g", [xl])
+    for p, out in ((32, T.W[:, S4 + 2048:S4 + 2176]), (64, T.Y[:, Y7 + 2048:Y7 + 2176]), (96, T.Y[:, Y11 + 2048:Y11 + 2176])):
+        lits = tok(g.partition_broadcast(out, T.litf[p:p + 1, :], 128), "cg")
+    dma("s", T.u0[0:16, :], T.u1[32:48, :], "dl0", [e1, fill])
+    dma("s", T.u6[112:128, :], T.u1[64:80, :], "du6")
+    dma("s", T.u7[48:64, :], T.u1[96:112, :], "du7")
     ship(0, T.W[0:1, S1:S1 + 2048], "sh0", s1)
-    nat(3, 2, "a", [zl], False)
-    t3 = lst(3, 2, "b", [], True)
+    x = cp(T.zf[:, 0:12], T.ptb[:, 128:140], [tz])
+    need("v", [x])
+    cp(T.zf[0:32, 3:4], T.px[0:32, 15:16])
+    zl = cp(T.zf[0:32, 7:8], T.px[0:32, 3:4])
+    nat(3, 2, "a", [], False)
+    t3 = lst(3, 2, "b", "ac", [zl], True)
     s2 = gather(T.W, S2, T.W, S1, S1 + 2176, T.u2, NV[1], s1 + [e2])
     e3 = cp(T.u3[:, :], T.p3[:, 0:128], [t3])
     ship(1, T.W[0:1, S2:S2 + 2048], "sh0", s2)
-    act(T.W[:, S4 + 2048:S4 + 2176], T.pta[:, 256:384])
-    lst(4, 3, "a1", [], False)
-    t4 = lst(4, 1, "b", [], True)
+    lst(4, 3, "a1", "ac3", [], False)
+    t4 = lst(4, 1, "b", "ac", [], True)
     s3 = gather(T.W, S3, T.W, S2, S2 + 2176, T.u3, NV[2], s2 + [e3])
-    act(T.Y[:, Y7 + 2048:Y7 + 2176], T.pta[:, 384:512])
-    e4 = ts(T.u4[:, :], T.p4[:, 0:128], T.pf[:, 9:10], None, OP.add, None, [t4])
+    e4 = ts(T.u4[:, :], T.p4[:, 0:128], off4, None, OP.add, None, [t4])
     dma("s", T.fl5[0:16, :], T.W[48:49, S3:S3 + 2048], "dl5", s3)
-    dma("s", T.fl6[48:64, :], T.W[80:81, S3:S3 + 2048], "dl6")
-    dma("s", T.fl7[96:112, :], T.W[112:113, S3:S3 + 2048], "dl7", [setup])
+    dma("s", T.fl6[32:48, :], T.W[80:81, S3:S3 + 2048], "dl6")
+    dma("s", T.fl7[80:96, :], T.W[112:113, S3:S3 + 2048], "dl7")
     ship(2, T.W[0:1, S3:S3 + 2048], "sh0", s3)
     s4 = gather(T.W, S4, T.W, S1, S3 + 2176, T.u4, NV[3], s3 + [e4])
     dma("s", T.Y[0:128:16, Y3:Y3 + 2048], T.W[0:8, S4:S4 + 2048], "dy3", s4 + [my3])
     dma("a", T.fl5[16:128, :], T.W[32:39, S4:S4 + 2048], "dl5", s4)
-    dma("s", T.fl6[64:128, :], T.W[64:68, S4:S4 + 2048], "dl6")
+    dma("s", T.fl6[48:112, :], T.W[64:68, S4:S4 + 2048], "dl6")
     dma("s", T.fl6[0:16, :], T.W[48:49, S4:S4 + 2048], "dl6")
-    dma("s", T.fl6[32:48, :], T.W[80:81, S4:S4 + 2048], "dl6")
-    dma("s", T.fl7[80:96, :], T.W[112:113, S4:S4 + 2048], "dl7")
-    dma("s", T.fl7[112:128, :], T.W[96:97, S4:S4 + 2048], "dl7")
+    dma("s", T.fl6[16:32, :], T.W[80:81, S4:S4 + 2048], "dl6")
+    dma("s", T.fl7[64:80, :], T.W[112:113, S4:S4 + 2048], "dl7")
+    dma("s", T.fl7[96:112, :], T.W[96:97, S4:S4 + 2048], "dl7")
     ship(3, T.W[0:1, S4:S4 + 2048], "sh0", s4)
-    e0 = cp(T.u0[0:16, :], T.fl0[0:16, :], al("dl0") + [my3])
-    s0 = gather(T.O, 0, T.W, S4, S4 + 2176, T.u0, NV[4], s4 + [e0])
-    act(T.Y[:, Y11 + 2048:Y11 + 2176], T.ptb[:, 0:128], [tz, zl])
+    s0 = gather(T.O, 0, T.W, S4, S4 + 2176, T.u0, NV[4], s4 + al("dl0") + [lits])
     ship(4, T.O[0:1, :], "sh2", s0)
     e5 = cp(T.u5[:, :], T.fl5[:, :], al("dl5"))
     s5 = gather(T.Y, Y7, T.Y, Y3, Y3 + 2432, T.u5, NV[5], al("dy3") + [e5])
-    e6 = ts(T.u6[:, :], T.fl6[:, :], T.pf[:, 10:11], None, OP.add, None, al("dl6"))
+    e6 = ts(T.u6[0:112, :], T.fl6[0:112, :], T.pf[0:112, 4:5], None, OP.add, None, al("dl6"))
     ship2(3, T.Y[0:32:16, Y7:Y7 + 2048], "sh1", s5)
-    s6 = gather(T.Y, Y11, T.Y, Y3, Y7 + 2432, T.u6, NV[6], s5 + [e6])
-    e7 = cp(T.u7[:, :], T.fl7[:, :], al("dl7"))
-    ship2(4, T.Y[16:48:16, Y11:Y11 + 2048], "sh2", s6)
-    ship2(5, T.Y[48:80:16, Y11:Y11 + 2048], "sh2", s6)
+    s6 = gather(T.Y, Y11, T.Y, Y7, Y3 + 2432, T.u6, NV[6], s5 + al("du6") + [e6])
+    e7 = cp(T.u7[64:112, :], T.fl7[64:112, :], al("dl7"))
+    ship2(5, T.Y[32:64:16, Y11:Y11 + 2048], "sh2", s6)
+    ship(8, T.Y[112:113, Y11:Y11 + 2048], "sh2", s6)
+    ship(9, T.Y[16:17, Y11:Y11 + 2048], "sh2", s6)
     ship(5, T.Y[0:1, Y11:Y11 + 2048], "sh2", s6)
-    s7 = gather(T.Y, YF, T.Y, Y11, Y11 + 2432, T.u7, NV[7], s6 + [e7])
-    ship2(6, T.Y[64:96:16, YF:YF + 2048], "sh3", s7)
-    ship2(7, T.Y[96:128:16, YF:YF + 2048], "sh3", s7, "a")
+    s7 = gather(T.Y, YF, T.Y, Y11, Y11 + 2432, T.u7, NV[7], s6 + al("du7") + [e7])
+    ship2(6, T.Y[48:80:16, YF:YF + 2048], "sh3", s7)
+    ship2(7, T.Y[80:112:16, YF:YF + 2048], "sh3", s7, "a")
     for c in range(4):
         send(c)
     a, b = engines_of(me)

@@ -1,10 +1,11 @@
 from concourse.bass import DstId, RemoteDMATransfer
 from concourse.mybir import AluOpType as OP, ActivationFunctionType as AF
 
-ID, S1, S2, S3, S4, WEND = 0, 2176, 4352, 6528, 8704, 10880
-Y7, Y3, Y11, YF, YEND = 0, 2432, 4864, 7296, 9344
+ID, S1, S2, S3, S4, WEND = 0, 2432, 4608, 6784, 8960, 11136
+Y7, Y11, YF, YEND = 0, 2432, 4864, 6912
 SYM = 2176
-NV = [40, 42, 42, 64, 64, 64, 64, 64]
+NV = [40, 40, 42, 32, 32, 60, 60, 64]
+NT = 6
 SCRATCH = {
     "stage": ("dram", [8, 128, 2], "int32"), "land": ("dram", [8, 128, 2], "int32"),
     "ost": ("dram", [8, 128, 32], "float32"), "yland": ("dram", [8, 128, 32], "float32"),
@@ -13,28 +14,21 @@ SCRATCH = {
     "first": ("sbuf", [128, 32], "float32"), "ones": ("sbuf", [128, 32], "float32"),
     "fi": ("sbuf", [128, 32], "int32"), "di": ("sbuf", [128, 32], "int32"),
     "qi": ("sbuf", [128, 224], "int32"), "qb": ("sbuf", [128, 224], "bfloat16"),
-    "pint": ("sbuf", [128, 8], "int32"), "pf": ("sbuf", [128, 16], "float32"), "zf": ("sbuf", [128, 16], "float32"),
-    "cb": ("sbuf", [128, 128 * 96], "bfloat16"),
-    "W": ("sbuf", [128, WEND], "float32"), "Y": ("sbuf", [128, YEND], "float32"), "O": ("sbuf", [128, 2048], "float32"),
+    "pint": ("sbuf", [128, 8], "int32"), "pf": ("sbuf", [128, 16], "float32"), "zf": ("sbuf", [128, 24], "float32"),
+    "cb": ("sbuf", [128, 128 * 112], "bfloat16"),
+    "W": ("sbuf", [128, WEND], "float32"), "Y": ("sbuf", [128, YEND], "float32"),
     "litx": ("sbuf", [128, 128], "int32"), "litf": ("sbuf", [128, 128], "float32"),
 }
-for _n in ("l5", "l6", "l7"):
-    SCRATCH["f" + _n] = ("sbuf", [128, 128], "float32")
-for _n in ("1", "2", "3", "4", "0", "5", "6", "7"):
+for _n in ("f1", "fl5", "fl6", "fl7"):
+    SCRATCH[_n] = ("sbuf", [128, 128], "float32")
+for _n in ("1", "2", "3", "4", "5", "6", "7"):
     SCRATCH["u" + _n] = ("sbuf", [128, 128], "uint16")
 for _n in ("p1", "p2", "p3", "p4", "px", "pta", "ptb"):
     SCRATCH[_n] = ("psum", [128, 512], "float32")
-SEMAPHORES = ["cv", "ca", "cp", "cg", "ld", "own", "arr", "lfr", "llit", "llx", "dl0", "du6", "du7", "dy3", "dl5", "dl6",
-              "dl7", "sh0", "sh1", "sh2", "sh3", "shown", "rloc", "yarr", "yst"]
-CALLS = [[0, 1], [3], [2, 4, 5], [6, 7]]
-
-
-def engines_of(r):
-    for grp in CALLS:
-        if r in grp:
-            n = 2 if len(grp) == 3 else 4
-            k = grp.index(r)
-            return k * n, k * n + n
+SEMAPHORES = ["cv", "ca", "cp", "cg", "ld", "own", "arr", "lfr", "llit", "llx", "dsel", "dpa", "dpb", "du5", "du6",
+              "du7", "dy3", "dl5", "dl6", "dl7", "sh0", "sh1", "sh2", "shown", "rloc", "yarr", "yst"]
+CALLS = [[0, 1], [2, 4, 5], [6, 7, 3]]
+NE = 4
 
 
 def rank_program(g, core, T, topo):
@@ -68,10 +62,13 @@ def rank_program(g, core, T, topo):
         k = slots[name]
         return T.cb[:, 128 * k:128 * k + 128]
 
-    def Cs(name, p1, c0, c1):
+    def Cp(name, p0, p1, c0, c1):
         C(name)
         k = 128 * slots[name]
-        return T.cb[0:p1, k + c0:k + c1]
+        return T.cb[p0:p1, k + c0:k + c1]
+
+    def Cs(name, p1, c0, c1):
+        return Cp(name, 0, p1, c0, c1)
 
     def ts(out, a, s1, s2, o0, o1=None, toks=()):
         need("v", toks)
@@ -96,7 +93,8 @@ def rank_program(g, core, T, topo):
             return tok(g.scalar.activation(out, a, AF.Identity, **kw), "ca")
         return tok(g.scalar.activation(out, a, AF.Copy), "ca")
 
-    def iota(out, pattern, base, ch):
+    def iota(out, pattern, base, ch, toks=()):
+        need("g", toks)
         return tok(g.iota(out, pattern, base, ch, allow_small_or_imprecise_dtypes=True), "cg")
 
     def mms(out, pairs, start, stop, toks):
@@ -111,13 +109,12 @@ def rank_program(g, core, T, topo):
     dma("a", T.land[me:me + 1, 0:32, :], T.frm[me:me + 1, :], "own")
     dma("s", T.land[me:me + 1, 32:64, :], T.ln[me:me + 1, :], "own")
     dma("a", T.land[me:me + 1, 64:128, :], T.lit[me:me + 1, :], "own")
-    for n in ("Gall", "Ga", "Gb", "Ga1", "Lb", "La1", "sa0", "sa9"):
+    ZT = ("selAll", "s03", "s46", "s57", "s0", "s1", "s2", "s3")
+    for n in ("Gall", "Gc", "Ga1", "Gb1", "La1", "Lb1") + ZT + ("ac3", "key3", "acb", "keyb"):
         C(n)
     kp = iota(T.pint[:, 0:1], [[0, 1]], 0, 1)
-    iota(C("tm"), [[0, 4], [100, 2], [1, 16]], 0, 0)
-    iota(C("tb"), [[2, 4], [0, 32]], 0, 0)
-    kt = iota(C("tab"), [[2, 4], [100, 2], [0, 16]], 0, 0)
-    kcc = iota(C("cc"), [[1, 128]], 0, 0)
+    iota(C("t16"), [[0, 8], [1, 16]], 0, 0)
+    kt = iota(C("tb"), [[2, 4], [0, 32]], 0, 0)
     need("g", al("ld"))
     trs = []
     for r in range(8):
@@ -130,77 +127,95 @@ def rank_program(g, core, T, topo):
     cnt["rloc"] = 7
     cnt["arr"] = 7
 
+    kid = iota(T.W[:, 0:256], [[1, 256]], 0, 0)
+    iota(Cs("n16", 16, 0, 128), [[16, 128]], 0, 0)
+    kn = iota(Cs("nk", 16, 0, 128), [[0, 128]], 0, 1)
+    x = iota(Cs("tg", 16, 0, 24), [[4, 4], [1, 6]], 0, 0)
+    need("g", [x])
+    iota(Cs("tg", 16, 4, 6), [[96, 2]], 3, 0)
+    iota(Cs("tg", 16, 10, 12), [[92, 2]], 7, 0)
+    iota(Cs("tg", 16, 16, 18), [[1, 2]], 9, 0)
+    ktg = iota(Cs("tg", 16, 22, 24), [[1, 2]], 13, 0)
+    kcc = iota(C("cc"), [[1, 128]], 0, 0)
+    x = iota(C("tabc"), [[2, 4], [100, 2], [0, 16]], 0, 0)
+    ktc = iota(Cs("tabc", 128, 0, 64), [[2, 2], [0, 32]], 0, 0, [x])
+    iota(C("ac3"), [[0, 16], [16, 8]], 0, 0)
+    x = iota(C("key3"), [[1, 16], [16, 8]], 0, 0)
+    iota(Cp("ac3", 32, 64, 0, 128), [[64, 2], [0, 16], [16, 4]], 0, 0, [x])
+    kk = iota(Cp("key3", 32, 64, 0, 128), [[64, 2], [1, 16], [16, 4]], 0, 0)
+    iota(Cs("l256", 16, 0, 128), [[0, 16], [256, 8]], 0, 0, [kk])
+    kl3 = iota(Cs("l16", 16, 0, 128), [[1, 16], [0, 8]], 0, 16)
+    iota(Cs("l256a", 16, 0, 128), [[1024, 2], [0, 16], [256, 4]], 0, 0)
+    kpl = iota(Cs("l16a", 16, 0, 128), [[0, 2], [1, 16], [0, 4]], 0, 16)
+
+    k0 = 128 * slots["Gall"]
+    ms(T.cb[:, k0:k0 + 512], -1.0)
+    bfill = ms(T.cb[:, k0 + 512:k0 + 768], 99.0)
+    zfill = ms(T.cb[0:16, k0 + 768:k0 + 128 * (6 + len(ZT))], 0.0)
+    p0, p2b, off4, code = [T.pf[:, i:i + 1] for i in range(4)]
+    pc = T.pf[0:16, 0:1]
+    x = cp(p0, T.pint[:, 0:1], [kp])
+    sall = ts(Cs("selAll", 16, 0, 128), Cs("t16", 16, 0, 128), pc, None, OP.is_equal, None, [x, zfill, kt])
+    for n, c0, c1 in (("s03", 0, 64), ("s46", 64, 80), ("s46", 96, 112), ("s57", 80, 96), ("s57", 112, 128),
+                      ("s0", 0, 16), ("s1", 16, 32), ("s2", 32, 48), ("s3", 48, 64)):
+        dma("s", Cs(n, 16, c0, c1), Cs("selAll", 16, c0, c1), "dsel", [sall])
+    ts(T.pint[:, 1:2], T.pint[:, 0:1], 5, None, OP.logical_shift_right)
+    x = ts(T.pint[:, 2:3], T.pint[:, 0:1], 4, 5, OP.logical_shift_right, OP.bitwise_and)
+    ts(p2b, T.pint[:, 1:2], 2.0, None, OP.mult, None, [x])
+    ts(off4, T.pint[:, 2:3], 5.0, float(S3 - S1), OP.is_lt, OP.mult)
+    b2 = ts(code, T.pint[:, 0:1], 32.0, 2176.0, OP.is_ge, OP.mult)
+    ts(C("mall"), C("tb"), p2b, None, OP.is_equal, None, [b2])
+
+    def block(n, b, c0, w):
+        return (Cp(n, 32 * b, 32 * b + 32, 32 * b + c0, 32 * b + c0 + w),
+                Cp("t16", 32 * b, 32 * b + 32, c0, c0 + w))
+    for b in range(4):
+        gdone = cp(*block("Gall", b, 0, 32))
+    for n, c0 in (("Gb1", 16), ("Lb1", 16), ("Ga1", 0), ("La1", 0)):
+        for b in range(4):
+            if n in ("Ga1", "Gb1") and b == 0:
+                ablk = act(*block(n, b, c0, 16), [bfill, kt], bias=0.5)
+            else:
+                ablk = act(*block(n, b, c0, 16), [bfill, kt])
+    ts(Cs("sel0", 8, 0, 128), Cs("tb", 8, 0, 128), T.pf[0:8, 0:1], None, OP.is_equal)
+    ts(Cs("sel1", 8, 0, 128), Cs("tb", 8, 0, 128), 1.0, T.pf[0:8, 0:1], OP.add, OP.is_equal)
+    ms(T.lnf[:, 0:1], 0.0)
+    ms(T.hf[:, 0:1], 0.0)
+    ms(T.ones[:, :], 1.0)
+    mlx = ms(T.litx[0:128, :], 0)
+    fill = ms(T.u7[:, :], 0)
+    tgs = ts(Cs("tgs", 16, 0, 24), Cs("tg", 16, 0, 24), pc, None, OP.is_equal, None, [ktg])
+
     need("s", al("arr", "own"))
     dma("s", T.ln2[0:16, :], T.land[:, 32:64, :], "lfr")
     dma("s", T.fr[0:16, :], T.land[:, 0:32, :], "lfr")
     dma("s", T.litr[0:8, :], T.land[:, 64:128, :], "llit")
+    dma("s", T.litx[32:128:32, :], T.land[2:8:2, 64:128, :], "llx", [mlx])
+    dma("s", T.litx[0:1, :], T.land[3:4, 64:128, :], "llx")
 
-    kid = iota(T.W[:, 0:256], [[1, 256]], 0, 0)
-    iota(Cs("n16", 16, 0, 128), [[16, 128]], 0, 0)
-    iota(Cs("nk", 16, 0, 128), [[0, 128]], 0, 1)
-    iota(Cs("l256", 16, 0, 128), [[0, 16], [256, 8]], 0, 0)
-    kpl = iota(Cs("l16", 16, 0, 128), [[1, 16], [0, 8]], 0, 16)
-    iota(C("ac"), [[0, 16], [16, 8]], 0, 0)
-    kk = iota(C("key"), [[1, 16], [16, 8]], 0, 0)
-    my3 = iota(T.Y[:, Y3:Y3 + 2176], [[0, 2176]], 0, 0)
-    ms(T.lnf[:, 0:1], 0.0)
-    ms(T.hf[:, 0:1], 0.0)
-    ms(T.ones[:, :], 1.0)
-    ms(T.cb[:, 0:512], -1.0)
-    ms(T.cb[:, 512:768], 99.0)
-    ms(T.cb[:, 768:1024], 0.0)
-    mlx = ms(T.litx[0:128, :], 0)
-    ms(T.u0[:, :], 0)
-    fill = ms(T.u7[:, :], 0)
-    p0, p2b, off4, code, off6 = [T.pf[:, i:i + 1] for i in range(5)]
-    ts(T.pint[:, 1:2], T.pint[:, 0:1], 5, None, OP.logical_shift_right, None, [kp])
-    x = ts(T.pint[:, 2:3], T.pint[:, 0:1], 4, 1, OP.logical_shift_right, OP.bitwise_and)
-    cp(p0, T.pint[:, 0:1])
-    ts(p2b, T.pint[:, 1:2], 2.0, None, OP.mult, None, [x])
-    ts(off4, T.pint[:, 2:3], 0.0, 4352.0, OP.is_equal, OP.mult)
-    ts(code, T.pint[:, 0:1], 32.0, 2176.0, OP.is_ge, OP.mult)
-    b2 = ts(off6, T.pint[:, 0:1], 16.0, 2432.0, OP.is_lt, OP.mult)
-    ts(Cs("selA", 16, 0, 128), Cs("tm", 16, 0, 128), T.pf[0:16, 0:1], None, OP.is_equal, None, [b2, kt])
-    x = ts(Cs("selB", 16, 0, 128), Cs("tm", 16, 0, 128), -100.0, T.pf[0:16, 0:1], OP.add, OP.is_equal)
-    ts(Cs("sel0", 8, 0, 128), Cs("tb", 8, 0, 128), T.pf[0:8, 0:1], None, OP.is_equal)
-    ts(Cs("sel1", 8, 0, 128), Cs("tb", 8, 0, 128), 1.0, T.pf[0:8, 0:1], OP.add, OP.is_equal)
-    ts(C("mall"), C("tb"), p2b, None, OP.is_equal)
-    ts(C("ma"), C("tab"), p2b, None, OP.is_equal)
-    need("v", [x])
-    cp(Cs("sa0", 16, 0, 16), Cs("selA", 16, 0, 16))
-    setup = cp(Cs("sa9", 16, 16, 128), Cs("selA", 16, 16, 128))
-
-    def block(n, b, c0):
-        k = 128 * slots[n] + 32 * b + c0
-        t = 128 * slots["tm"]
-        out, src = T.cb[32 * b:32 * b + 32, k:k + 16], T.cb[32 * b:32 * b + 32, t:t + 16]
-        if n == "Ga1" and b == 0:
-            return ts(out, src, 0.5, None, OP.add)
-        return cp(out, src)
-    for n, c0 in (("Gall", 0), ("Gall", 16), ("Ga", 0), ("Gb", 16), ("Lb", 16), ("Ga1", 0), ("La1", 0)):
-        for b in range(4):
-            gdone = block(n, b, c0)
-    x = cp(C("ac3"), C("ac"), [kk])
-    need("v", [x])
-    cp(Cs("ac3", 32, 0, 128), Cs("cc", 32, 0, 128), [kcc])
+    dma("s", Cs("ac3", 32, 0, 128), Cs("cc", 32, 0, 128), "dpa", [kcc, kk])
+    dma("s", Cp("acb", 32, 64, 0, 64), Cp("ac3", 32, 64, 64, 128), "dpb")
+    dma("s", Cp("acb", 32, 64, 64, 128), Cp("ac3", 32, 64, 0, 64), "dpb")
+    dma("s", Cp("acb", 0, 32, 0, 64), Cp("cc", 0, 32, 64, 128), "dpb")
+    dma("s", Cp("acb", 0, 32, 64, 128), Cp("cc", 0, 32, 0, 64), "dpb")
+    dma("s", Cp("keyb", 0, 64, 0, 64), Cp("key3", 0, 64, 64, 128), "dpb")
+    dma("s", Cp("keyb", 0, 64, 64, 128), Cp("key3", 0, 64, 0, 64), "dpb")
+    k1, k2 = 128 * slots["ac3"], 128 * slots["acb"]
+    dma("s", T.cb[64:128, k2:k2 + 256], T.cb[64:128, k1:k1 + 256], "dpb")
+    for a, b in (("n16r", "n16"), ("l256r", "l256a")):
+        dma("s", Cs(a, 16, 0, 64), Cs(b, 16, 64, 128), "dpb", [kpl])
+        dma("s", Cs(a, 16, 64, 128), Cs(b, 16, 0, 64), "dpb")
 
     x = act(T.W[:, 256:512], T.W[:, 0:256], [kid], bias=256.0)
     x = act(T.W[:, 512:1024], T.W[:, 0:512], [x], bias=512.0)
     i2 = act(T.W[:, 1024:2048], T.W[:, 0:1024], [x], bias=1024.0)
-    for y in (Y3, Y7, Y11):
-        act(T.Y[:, y + SYM:y + SYM + 256], T.W[:, 0:256])
 
     P = {n: T["p%d" % n][:, 0:128] for n in (1, 2, 3, 4)}
 
-    def place(n, nats, lists):
-        mms(P[n], [(Cs(w, 16, 0, 128), Cs(q, 16, 0, 128)) for w in nats for q in ("n16", "nk")] +
-            [(Cs(w, 16, 0, 128), Cs(q, 16, 0, 128)) for w in lists for q in ("l256", "l16")], True, False, [setup, kpl])
-    place(1, ("selA", "selB"), ())
-    place(2, ("selA", "selB"), ())
-    place(3, ("selA",), ("selB",))
-    place(4, ("sa0",), ("sa9", "selB"))
-
-    dma("s", T.litx[32:128:32, :], T.land[2:8:2, 64:128, :], "llx", [mlx])
+    def place(n, parts, toks):
+        mms(P[n], [(Cs(w, 16, 0, 128), Cs(q, 16, 0, 128)) for w, a, b in parts for q in (a, b)], True, False, toks)
+    place(1, (("selAll", "n16", "nk"),), [sall, kn])
+    place(2, (("selAll", "n16", "nk"),), [])
 
     n1 = cp(T.lnf[0:16, 1:33], T.ln2[0:16, :], al("lfr"))
     n2 = tt(T.hf[0:16, 1:33], T.fr[0:16, :], T.ln2[0:16, :], OP.add)
@@ -217,15 +232,18 @@ def rank_program(g, core, T, topo):
     q1 = ts(Q(1), T.fi[0:16, :], 4, None, OP.logical_shift_right)
     x = cp(T.qb[0:16, 0:128], T.qi[0:16, 0:128], [q1])
 
-    def turn(dst, ks, toks):
+    def turn(dst, c0, ks, toks):
         need("p", toks)
         for i, k in enumerate(ks):
             for b in range(4):
-                ins = g.tensor.matmul(dst[32 * b:32 * b + 32, 4 * i:4 * i + 4], T.qb[0:16, 32 * k:32 * k + 32],
-                                      Cs("selA", 16, 4 * b, 4 * b + 4), True, True)
+                ins = g.tensor.matmul(dst[32 * b:32 * b + 32, c0 + NT * i:c0 + NT * i + NT],
+                                      T.qb[0:16, 32 * k:32 * k + 32], Cs("tgs", 16, NT * b, NT * b + NT), True, True)
         return tok(ins, "cp")
-    zz = turn(T.px[:, 0:16], (1, 2, 3, 0), [x])
+    zz = turn(T.px, 0, (1, 2, 3, 0), [x, tgs])
     nl = cp(Cs("lit", 8, 0, 128), T.litr[0:8, :], al("llit"))
+    for b in range(4):
+        cp(*block("Gc", b, 0, 32 if b < 2 else 16))
+    setup = ts(C("mc"), C("tabc"), p2b, None, OP.is_equal, None, [ktc])
     need("p", [nl])
     for k, n in enumerate(("sel0", "sel1")):
         ins = g.tensor.matmul(T.pta[:, 128 * k:128 * k + 128], Cs(n, 8, 0, 128), Cs("lit", 8, 0, 128), True, True)
@@ -236,10 +254,10 @@ def rank_program(g, core, T, topo):
     tails = act(T.W[:, S3 + 2048:S3 + 2176], T.pta[:, 128:256], bias=code)
 
     def X(k, t):
-        return T.px[:, 4 * k + t:4 * k + t + 1]
+        return T.px[:, NT * k + t:NT * k + t + 1]
 
     def Z(k, t):
-        return T.zf[:, 4 * k + t:4 * k + t + 1]
+        return T.zf[:, NT * k + t:NT * k + t + 1]
 
     def nat(n, t, m, toks, stop):
         need("v", toks)
@@ -253,30 +271,31 @@ def rank_program(g, core, T, topo):
             y = mms(P[n], [(C("nl" + w), C("n2" + w + str(h)))], False, stop and h == 1, [x])
         return y
 
-    def lst(n, t, m, row, toks, stop):
+    def lst(n, t, m, row, key, toks, stop):
         need("v", toks)
         w = "%d%s" % (t, m)
         for k, (r, z, op, side, lop) in enumerate(((row, 1, OP.is_gt, "L", OP.is_lt), (row, 1, OP.is_ge, "G", OP.is_gt),
-                                                   ("key", 2, OP.is_ge, "G", OP.is_equal))):
+                                                   (key, 2, OP.is_ge, "G", OP.is_equal))):
             ts(C("ql%d%s" % (k, w)), C(side + m), Z(0, t), None, lop)
             for h in (0, 1):
                 x = ts(C("q%d%s%d" % (k, w, h)), C(r), Z(z, t), X(1 + h, t), op, OP.mult)
                 y = mms(P[n], [(C("ql%d%s" % (k, w)), C("q%d%s%d" % (k, w, h)))], False, stop and k == 2 and h == 1, [x])
         return y
 
-    def gather(out, o0, win, w0, w1, lu, nv, toks):
+    def gather(out, o0, win, w0, w1, lu, nv, toks, c0=0, c1=128):
         need("v", toks)
-        tv = tok(g.vector.tensor_copy(out[:, o0:o0 + 16 * nv], win[:, w0:w1].indirect(lu[:, 0:nv])), "cv")
+        cm = c0 + nv
+        tv = tok(g.vector.tensor_copy(out[:, o0 + 16 * c0:o0 + 16 * cm], win[:, w0:w1].indirect(lu[:, c0:cm])), "cv")
         need("a", toks)
-        ta = tok(g.scalar.activation(out[:, o0 + 16 * nv:o0 + 2048], win[:, w0:w1].indirect(lu[:, nv:128]), AF.Copy), "ca")
+        ta = tok(g.scalar.activation(out[:, o0 + 16 * cm:o0 + 16 * c1], win[:, w0:w1].indirect(lu[:, cm:c1]), AF.Copy), "ca")
         return [tv, ta]
 
-    def ship(v, src, sem, toks):
+    def ship(v, src, sem, toks, q="s"):
         r, k = v // 2, v % 2
         if r == me:
-            dma("s", T.y[me:me + 1, 2048 * k:2048 * k + 2048], src, "shown", toks)
+            dma(q, T.y[me:me + 1, 2048 * k:2048 * k + 2048], src, "shown", toks)
         else:
-            dma("s", T.ost[r:r + 1, 64 * k:64 * k + 64, :], src, sem, toks)
+            dma(q, T.ost[r:r + 1, 64 * k:64 * k + 64, :], src, sem, toks)
 
     def ship2(r, src, sem, toks, q="s"):
         if r == me:
@@ -285,84 +304,99 @@ def rank_program(g, core, T, topo):
             dma(q, T.ost[r:r + 1, :, :], src, sem, toks)
 
     def send(c):
-        trs = []
+        trs, used = [], []
         for r in CALLS[c]:
             if r != me:
                 rid, pid = topo.addr(T.cores[r])[:2]
-                a, b = engines_of(r)
-                m = 0
-                for e in topo.engines(core, T.cores[r])[a:b]:
-                    m |= 1 << e
-                trs.append(RemoteDMATransfer(dst_ids=[DstId(rid=rid, pnc=pid)], dma_engine_mask=m,
+                e = topo.engines(core, T.cores[r])
+                if topo.chip(core) == topo.chip(T.cores[r]):
+                    e = e[::-1]
+                e = [i for i in e if i not in used][:NE]
+                used.extend(e)
+                trs.append(RemoteDMATransfer(dst_ids=[DstId(rid=rid, pnc=pid)], dma_engine_mask=sum(1 << i for i in e),
                                              remote_sem=T.sem.yarr, src=T.ost[r], dst=T.yland[me]))
-                cnt["rloc"] += b - a
+                cnt["rloc"] += NE
         if trs:
             need("g", al("sh%d" % c))
             g.remote_dma_fused(trs, local_sem=T.sem.rloc)
 
-    t1 = nat(1, 0, "all", [zz, gdone], True)
+    t1 = nat(1, 0, "all", [zz, gdone, kcc], True)
     ts(Q(4), Q(1), 15, None, OP.bitwise_and)
     x = ts(Q(5), T.fi[0:16, :], 4, 112, OP.logical_shift_right, OP.bitwise_and)
     x = tt(Q(6), Q(5), Q(0), OP.add, [x])
     e1 = cp(T.u1[:, :], T.p1[:, 0:128], [t1])
     x = cp(T.qb[0:16, 128:224], T.qi[0:16, 128:224], [x])
     t2 = nat(2, 1, "all", [], True)
-    tz = turn(T.ptb[:, 128:140], (4, 5, 6), [x])
+    tz = turn(T.ptb, 128, (4, 5, 6), [x])
+    place(3, (("s03", "n16", "nk"), ("s46", "n16", "nk"), ("s57", "l256", "l16")), [kl3] + al("dsel"))
     s1 = gather(T.W, S1, T.W, ID, ID + 2176, T.u1, NV[0], [e1, i2, tails])
     e2 = cp(T.u2[:, :], T.p2[:, 0:128], [t2])
-    xl = cp(T.litf[:, :], T.litx[:, :], al("llx"))
-    need("g", [xl])
-    for p, out in ((32, T.W[:, S4 + 2048:S4 + 2176]), (64, T.Y[:, Y7 + 2048:Y7 + 2176]), (96, T.Y[:, Y11 + 2048:Y11 + 2176])):
-        lits = tok(g.partition_broadcast(out, T.litf[p:p + 1, :], 128), "cg")
-    dma("s", T.u0[0:16, :], T.u1[32:48, :], "dl0", [e1, fill])
-    dma("s", T.u6[112:128, :], T.u1[64:80, :], "du6")
+    dma("s", T.u5[112:128, :], T.u1[32:48, :], "du5", [e1, fill])
     dma("s", T.u7[48:64, :], T.u1[96:112, :], "du7")
     ship(0, T.W[0:1, S1:S1 + 2048], "sh0", s1)
-    x = cp(T.zf[:, 0:12], T.ptb[:, 128:140], [tz])
+    dma("s", T.u6[112:128, :], T.u2[32:48, :], "du6", [e2])
+    xl = cp(T.litf[:, :], T.litx[:, :], al("llx"))
+
+    def lits(out, p, n, toks):
+        need("g", toks)
+        return tok(g.partition_broadcast(out, T.litf[p:p + 1, :], n), "cg")
+    iota(T.W[:, ID + SYM:ID + SYM + 256], [[1, 256]], 0, 0, al("cg"))
+    l5 = lits(T.W[:, ID + 2048:ID + 2176], 32, 128, [xl] + s1)
+    iota(T.Y[:, Y7 + SYM:Y7 + SYM + 256], [[1, 256]], 0, 0, al("cg"))
+    x = lits(T.Y[:, Y7 + 2048:Y7 + 2176], 32, 128, al("cg"))
+    l6 = lits(T.Y[0:16, Y7 + 2048:Y7 + 2176], 64, 16, [x])
+    iota(T.Y[:, Y11 + SYM:Y11 + SYM + 256], [[1, 256]], 0, 0, al("cg"))
+    x = lits(T.Y[:, Y11 + 2048:Y11 + 2176], 0, 128, al("cg"))
+    l7 = lits(T.Y[0:64, Y11 + 2048:Y11 + 2176], 96, 64, [x])
+    x = cp(T.zf[:, 0:3 * NT], T.ptb[:, 128:128 + 3 * NT], [tz])
     need("v", [x])
-    cp(T.zf[0:32, 3:4], T.px[0:32, 15:16])
-    zl = cp(T.zf[0:32, 7:8], T.px[0:32, 3:4])
-    nat(3, 2, "a", [], False)
-    t3 = lst(3, 2, "b", "ac", [zl], True)
+    cp(T.zf[0:32, 3:5], T.px[0:32, 3 * NT + 3:3 * NT + 5])
+    zl = cp(T.zf[0:32, NT + 3:NT + 5], T.px[0:32, 3:5])
+    nat(3, 2, "c", [setup], False)
+    t3 = lst(3, 5, "b1", "ac3", "key3", [zl, ablk, kk] + al("dpa"), True)
+    place(4, (("s0", "n16", "nk"), ("s1", "n16r", "nk"), ("s2", "l256a", "l16a"), ("s3", "l256r", "l16a"),
+              ("s46", "l256", "l16"), ("s57", "l256", "l16")), [kpl] + al("dpb"))
     s2 = gather(T.W, S2, T.W, S1, S1 + 2176, T.u2, NV[1], s1 + [e2])
     e3 = cp(T.u3[:, :], T.p3[:, 0:128], [t3])
     ship(1, T.W[0:1, S2:S2 + 2048], "sh0", s2)
-    lst(4, 3, "a1", "ac3", [], False)
-    t4 = lst(4, 1, "b", "ac", [], True)
+    lst(4, 3, "a1", "ac3", "key3", [], False)
+    t4 = lst(4, 4, "b1", "acb", "keyb", al("dpb"), True)
     s3 = gather(T.W, S3, T.W, S2, S2 + 2176, T.u3, NV[2], s2 + [e3])
     e4 = ts(T.u4[:, :], T.p4[:, 0:128], off4, None, OP.add, None, [t4])
-    dma("s", T.fl5[0:16, :], T.W[48:49, S3:S3 + 2048], "dl5", s3)
-    dma("s", T.fl6[32:48, :], T.W[80:81, S3:S3 + 2048], "dl6")
+    dma("s", T.u7[112:128, :], T.u3[32:48, :], "du7", [e3])
+    dma("s", T.fl6[32:48, :], T.W[80:81, S3:S3 + 2048], "dl6", s3)
     dma("s", T.fl7[80:96, :], T.W[112:113, S3:S3 + 2048], "dl7")
     ship(2, T.W[0:1, S3:S3 + 2048], "sh0", s3)
-    s4 = gather(T.W, S4, T.W, S1, S3 + 2176, T.u4, NV[3], s3 + [e4])
-    dma("s", T.Y[0:128:16, Y3:Y3 + 2048], T.W[0:8, S4:S4 + 2048], "dy3", s4 + [my3])
-    dma("a", T.fl5[16:128, :], T.W[32:39, S4:S4 + 2048], "dl5", s4)
-    dma("s", T.fl6[48:112, :], T.W[64:68, S4:S4 + 2048], "dl6")
-    dma("s", T.fl6[0:16, :], T.W[48:49, S4:S4 + 2048], "dl6")
+    s4 = gather(T.W, S4, T.W, S1, S3 + 2176, T.u4, NV[3], s3 + [e4], 0, 64)
+    dma("s", T.fl5[0:112, 0:64], T.W[32:39, S4:S4 + 1024], "dl5", s4)
+    dma("s", T.fl5[0:112, 64:128], T.W[48:55, S4:S4 + 1024], "dl5")
+    dma("s", T.W[0:128:16, ID:ID + 1024], T.W[0:8, S4:S4 + 1024], "dy3")
+    dma("s", T.W[0:128:16, ID + 1024:ID + 2048], T.W[16:24, S4:S4 + 1024], "dy3")
+    s4 = gather(T.W, S4, T.W, S1, S3 + 2176, T.u4, NV[4], s3 + [e4], 64, 128)
+    f1 = cp(T.f1[64:96, :], T.u1[64:96, :])
+    dma("s", T.fl6[48:112, :], T.W[64:68, S4:S4 + 2048], "dl6", s4)
     dma("s", T.fl6[16:32, :], T.W[80:81, S4:S4 + 2048], "dl6")
+    dma("s", T.fl6[0:16, :], T.f1[64:80, :], "dl6", [f1])
     dma("s", T.fl7[64:80, :], T.W[112:113, S4:S4 + 2048], "dl7")
     dma("s", T.fl7[96:112, :], T.W[96:97, S4:S4 + 2048], "dl7")
     ship(3, T.W[0:1, S4:S4 + 2048], "sh0", s4)
-    s0 = gather(T.O, 0, T.W, S4, S4 + 2176, T.u0, NV[4], s4 + al("dl0") + [lits])
-    ship(4, T.O[0:1, :], "sh2", s0)
-    e5 = cp(T.u5[:, :], T.fl5[:, :], al("dl5"))
-    s5 = gather(T.Y, Y7, T.Y, Y3, Y3 + 2432, T.u5, NV[5], al("dy3") + [e5])
-    e6 = ts(T.u6[0:112, :], T.fl6[0:112, :], T.pf[0:112, 4:5], None, OP.add, None, al("dl6"))
-    ship2(3, T.Y[0:32:16, Y7:Y7 + 2048], "sh1", s5)
-    s6 = gather(T.Y, Y11, T.Y, Y7, Y3 + 2432, T.u6, NV[6], s5 + al("du6") + [e6])
+    e5 = cp(T.u5[0:112, :], T.fl5[0:112, :], al("dl5"))
+    s5 = gather(T.Y, Y7, T.W, ID, ID + 2432, T.u5, NV[5], al("dy3", "du5") + [e5, l5])
+    e6 = cp(T.u6[0:112, :], T.fl6[0:112, :], al("dl6"))
+    ship(4, T.Y[112:113, Y7:Y7 + 2048], "sh1", s5)
+    ship(7, T.Y[0:1, Y7:Y7 + 2048], "sh2", s5)
+    s6 = gather(T.Y, Y11, T.Y, Y7, Y7 + 2432, T.u6, NV[6], s5 + al("du6") + [e6, l6])
     e7 = cp(T.u7[64:112, :], T.fl7[64:112, :], al("dl7"))
-    ship2(5, T.Y[32:64:16, Y11:Y11 + 2048], "sh2", s6)
-    ship(8, T.Y[112:113, Y11:Y11 + 2048], "sh2", s6)
-    ship(9, T.Y[16:17, Y11:Y11 + 2048], "sh2", s6)
-    ship(5, T.Y[0:1, Y11:Y11 + 2048], "sh2", s6)
-    s7 = gather(T.Y, YF, T.Y, Y11, Y11 + 2432, T.u7, NV[7], s6 + al("du7") + [e7])
-    ship2(6, T.Y[48:80:16, YF:YF + 2048], "sh3", s7)
-    ship2(7, T.Y[80:112:16, YF:YF + 2048], "sh3", s7, "a")
-    for c in range(4):
+    ship2(4, T.Y[0:32:16, Y11:Y11 + 2048], "sh1", s6)
+    ship2(5, T.Y[32:64:16, Y11:Y11 + 2048], "sh1", s6)
+    ship(5, T.Y[112:113, Y11:Y11 + 2048], "sh1", s6)
+    s7 = gather(T.Y, YF, T.Y, Y11, Y11 + 2432, T.u7, NV[7], s6 + al("du7") + [e7, l7])
+    ship2(6, T.Y[48:80:16, YF:YF + 2048], "sh2", s7)
+    ship2(7, T.Y[80:112:16, YF:YF + 2048], "sh2", s7, "a")
+    ship(6, T.Y[112:113, YF:YF + 2048], "sh2", s7)
+    for c in range(3):
         send(c)
-    a, b = engines_of(me)
-    cnt["yarr"] = 7 * (b - a)
+    cnt["yarr"] = 7 * NE
     if me > 0:
         dma("s", T.y[0:me, :], T.yland[0:me, :, :], "yst", al("yarr"))
     if me < 7:

from concourse.bass import DstId, RemoteDMATransfer
from concourse.mybir import AluOpType as OP, ActivationFunctionType as AF

ID, S1, S2, S3, S4, WEND = 0, 2432, 4608, 6784, 8960, 11136
Y7, Y11, YF, YEND = 0, 2432, 4864, 6912
SYM = 2176
NV = [40, 40, 42, 32, 32, 60, 60, 64]
NT = 6
SCRATCH = {
    "stage": ("dram", [8, 128, 2], "int32"), "land": ("dram", [8, 128, 2], "int32"),
    "ost": ("dram", [8, 128, 32], "float32"), "yland": ("dram", [8, 128, 32], "float32"),
    "fr": ("sbuf", [128, 32], "int32"), "ln2": ("sbuf", [128, 32], "int32"), "litr": ("sbuf", [128, 128], "int32"),
    "lnf": ("sbuf", [128, 40], "float32"), "hf": ("sbuf", [128, 40], "float32"),
    "first": ("sbuf", [128, 32], "float32"), "ones": ("sbuf", [128, 32], "float32"),
    "fi": ("sbuf", [128, 32], "int32"), "di": ("sbuf", [128, 32], "int32"),
    "qi": ("sbuf", [128, 224], "int32"), "qb": ("sbuf", [128, 224], "bfloat16"),
    "pint": ("sbuf", [128, 8], "int32"), "pf": ("sbuf", [128, 16], "float32"), "zf": ("sbuf", [128, 24], "float32"),
    "cb": ("sbuf", [128, 128 * 112], "bfloat16"),
    "W": ("sbuf", [128, WEND], "float32"), "Y": ("sbuf", [128, YEND], "float32"),
    "litx": ("sbuf", [128, 128], "int32"), "litf": ("sbuf", [128, 128], "float32"),
}
for _n in ("f1", "fl5", "fl6", "fl7"):
    SCRATCH[_n] = ("sbuf", [128, 128], "float32")
for _n in ("1", "2", "3", "4", "5", "6", "7"):
    SCRATCH["u" + _n] = ("sbuf", [128, 128], "uint16")
for _n in ("p1", "p2", "p3", "p4", "px", "pta", "ptb"):
    SCRATCH[_n] = ("psum", [128, 512], "float32")
SEMAPHORES = ["cv", "ca", "cp", "cg", "ld", "own", "arr", "lfr", "llit", "llx", "dsel", "dpa", "dpb", "du5", "du6",
              "du7", "dy3", "dl5", "dl6", "dl7", "sh0", "sh1", "sh2", "shown", "rloc", "yarr", "yst"]
CALLS = [[0, 1], [2, 4, 5], [6, 7, 3]]
NE = 4


def rank_program(g, core, T, topo):
    me = T.rank_of(core)
    if me is None:
        return
    eng = {"v": g.vector, "a": g.scalar, "p": g.tensor, "g": g, "s": g.sync}
    cnt, seen, slots = {}, {}, {}

    def need(q, toks):
        for sem, val in toks:
            if seen.get((q, sem), 0) < val:
                eng[q].wait_ge(T.sem[sem], val)
                seen[(q, sem)] = val

    def tok(ins, sem, n=1):
        cnt[sem] = cnt.get(sem, 0) + n
        ins.then_inc(T.sem[sem], n)
        return (sem, cnt[sem])

    def al(*sems):
        return [(s, cnt[s]) for s in sems]

    def dma(q, out, in_, sem, toks=()):
        need(q, toks)
        return tok(eng[q].dma_start(out=out, in_=in_), sem, 16)

    def C(name):
        if name not in slots:
            slots[name] = len(slots)
        k = slots[name]
        return T.cb[:, 128 * k:128 * k + 128]

    def Cp(name, p0, p1, c0, c1):
        C(name)
        k = 128 * slots[name]
        return T.cb[p0:p1, k + c0:k + c1]

    def Cs(name, p1, c0, c1):
        return Cp(name, 0, p1, c0, c1)

    def ts(out, a, s1, s2, o0, o1=None, toks=()):
        need("v", toks)
        if o1 is None:
            return tok(g.vector.tensor_scalar(out, a, s1, None, o0), "cv")
        return tok(g.vector.tensor_scalar(out, a, s1, s2, o0, o1), "cv")

    def tt(out, a, b, op, toks=()):
        need("v", toks)
        return tok(g.vector.tensor_tensor(out, a, b, op), "cv")

    def cp(out, a, toks=()):
        need("v", toks)
        return tok(g.vector.tensor_copy(out, a), "cv")

    def ms(out, x):
        return tok(g.vector.memset(out, x), "cv")

    def act(out, a, toks=(), **kw):
        need("a", toks)
        if kw:
            return tok(g.scalar.activation(out, a, AF.Identity, **kw), "ca")
        return tok(g.scalar.activation(out, a, AF.Copy), "ca")

    def iota(out, pattern, base, ch, toks=()):
        need("g", toks)
        return tok(g.iota(out, pattern, base, ch, allow_small_or_imprecise_dtypes=True), "cg")

    def mms(out, pairs, start, stop, toks):
        need("p", toks)
        for n, (l, r) in enumerate(pairs):
            ins = g.tensor.matmul(out, l, r, start and n == 0, stop and n == len(pairs) - 1)
        return tok(ins, "cp")

    dma("s", T.stage[:, 0:32, :], T.frm[:, :], "ld")
    dma("a", T.stage[:, 32:64, :], T.ln[:, :], "ld")
    dma("s", T.stage[:, 64:128, :], T.lit[:, :], "ld")
    dma("a", T.land[me:me + 1, 0:32, :], T.frm[me:me + 1, :], "own")
    dma("s", T.land[me:me + 1, 32:64, :], T.ln[me:me + 1, :], "own")
    dma("a", T.land[me:me + 1, 64:128, :], T.lit[me:me + 1, :], "own")
    ZT = ("selAll", "s03", "s46", "s57", "s0", "s1", "s2", "s3")
    for n in ("Gall", "Gc", "Ga1", "Gb1", "La1", "Lb1") + ZT + ("ac3", "key3", "acb", "keyb"):
        C(n)
    kp = iota(T.pint[:, 0:1], [[0, 1]], 0, 1)
    iota(C("t16"), [[0, 8], [1, 16]], 0, 0)
    kt = iota(C("tb"), [[2, 4], [0, 32]], 0, 0)
    need("g", al("ld"))
    trs = []
    for r in range(8):
        if r != me:
            rid, pid = topo.addr(T.cores[r])[:2]
            e = topo.engines(core, T.cores[r])
            trs.append(RemoteDMATransfer(dst_ids=[DstId(rid=rid, pnc=pid)], dma_engine_mask=1 << e[len(trs)],
                                         remote_sem=T.sem.arr, src=T.stage[r], dst=T.land[me]))
    g.remote_dma_fused(trs, local_sem=T.sem.rloc)
    cnt["rloc"] = 7
    cnt["arr"] = 7

    kid = iota(T.W[:, 0:256], [[1, 256]], 0, 0)
    iota(Cs("n16", 16, 0, 128), [[16, 128]], 0, 0)
    kn = iota(Cs("nk", 16, 0, 128), [[0, 128]], 0, 1)
    x = iota(Cs("tg", 16, 0, 24), [[4, 4], [1, 6]], 0, 0)
    need("g", [x])
    iota(Cs("tg", 16, 4, 6), [[96, 2]], 3, 0)
    iota(Cs("tg", 16, 10, 12), [[92, 2]], 7, 0)
    iota(Cs("tg", 16, 16, 18), [[1, 2]], 9, 0)
    ktg = iota(Cs("tg", 16, 22, 24), [[1, 2]], 13, 0)
    kcc = iota(C("cc"), [[1, 128]], 0, 0)
    x = iota(C("tabc"), [[2, 4], [100, 2], [0, 16]], 0, 0)
    ktc = iota(Cs("tabc", 128, 0, 64), [[2, 2], [0, 32]], 0, 0, [x])
    iota(C("ac3"), [[0, 16], [16, 8]], 0, 0)
    x = iota(C("key3"), [[1, 16], [16, 8]], 0, 0)
    iota(Cp("ac3", 32, 64, 0, 128), [[64, 2], [0, 16], [16, 4]], 0, 0, [x])
    kk = iota(Cp("key3", 32, 64, 0, 128), [[64, 2], [1, 16], [16, 4]], 0, 0)
    iota(Cs("l256", 16, 0, 128), [[0, 16], [256, 8]], 0, 0, [kk])
    kl3 = iota(Cs("l16", 16, 0, 128), [[1, 16], [0, 8]], 0, 16)
    iota(Cs("l256a", 16, 0, 128), [[1024, 2], [0, 16], [256, 4]], 0, 0)
    kpl = iota(Cs("l16a", 16, 0, 128), [[0, 2], [1, 16], [0, 4]], 0, 16)

    k0 = 128 * slots["Gall"]
    ms(T.cb[:, k0:k0 + 512], -1.0)
    bfill = ms(T.cb[:, k0 + 512:k0 + 768], 99.0)
    zfill = ms(T.cb[0:16, k0 + 768:k0 + 128 * (6 + len(ZT))], 0.0)
    p0, p2b, off4, code = [T.pf[:, i:i + 1] for i in range(4)]
    pc = T.pf[0:16, 0:1]
    x = cp(p0, T.pint[:, 0:1], [kp])
    sall = ts(Cs("selAll", 16, 0, 128), Cs("t16", 16, 0, 128), pc, None, OP.is_equal, None, [x, zfill, kt])
    for n, c0, c1 in (("s03", 0, 64), ("s46", 64, 80), ("s46", 96, 112), ("s57", 80, 96), ("s57", 112, 128),
                      ("s0", 0, 16), ("s1", 16, 32), ("s2", 32, 48), ("s3", 48, 64)):
        dma("s", Cs(n, 16, c0, c1), Cs("selAll", 16, c0, c1), "dsel", [sall])
    ts(T.pint[:, 1:2], T.pint[:, 0:1], 5, None, OP.logical_shift_right)
    x = ts(T.pint[:, 2:3], T.pint[:, 0:1], 4, 5, OP.logical_shift_right, OP.bitwise_and)
    ts(p2b, T.pint[:, 1:2], 2.0, None, OP.mult, None, [x])
    ts(off4, T.pint[:, 2:3], 5.0, float(S3 - S1), OP.is_lt, OP.mult)
    b2 = ts(code, T.pint[:, 0:1], 32.0, 2176.0, OP.is_ge, OP.mult)
    ts(C("mall"), C("tb"), p2b, None, OP.is_equal, None, [b2])

    def block(n, b, c0, w):
        return (Cp(n, 32 * b, 32 * b + 32, 32 * b + c0, 32 * b + c0 + w),
                Cp("t16", 32 * b, 32 * b + 32, c0, c0 + w))
    for b in range(4):
        gdone = cp(*block("Gall", b, 0, 32))
    for n, c0 in (("Gb1", 16), ("Lb1", 16), ("Ga1", 0), ("La1", 0)):
        for b in range(4):
            if n in ("Ga1", "Gb1") and b == 0:
                ablk = act(*block(n, b, c0, 16), [bfill, kt], bias=0.5)
            else:
                ablk = act(*block(n, b, c0, 16), [bfill, kt])
    ts(Cs("sel0", 8, 0, 128), Cs("tb", 8, 0, 128), T.pf[0:8, 0:1], None, OP.is_equal)
    ts(Cs("sel1", 8, 0, 128), Cs("tb", 8, 0, 128), 1.0, T.pf[0:8, 0:1], OP.add, OP.is_equal)
    ms(T.lnf[:, 0:1], 0.0)
    ms(T.hf[:, 0:1], 0.0)
    ms(T.ones[:, :], 1.0)
    mlx = ms(T.litx[0:128, :], 0)
    fill = ms(T.u7[:, :], 0)
    tgs = ts(Cs("tgs", 16, 0, 24), Cs("tg", 16, 0, 24), pc, None, OP.is_equal, None, [ktg])

    need("s", al("arr", "own"))
    dma("s", T.ln2[0:16, :], T.land[:, 32:64, :], "lfr")
    dma("s", T.fr[0:16, :], T.land[:, 0:32, :], "lfr")
    dma("s", T.litr[0:8, :], T.land[:, 64:128, :], "llit")
    dma("s", T.litx[32:128:32, :], T.land[2:8:2, 64:128, :], "llx", [mlx])
    dma("s", T.litx[0:1, :], T.land[3:4, 64:128, :], "llx")

    dma("s", Cs("ac3", 32, 0, 128), Cs("cc", 32, 0, 128), "dpa", [kcc, kk])
    dma("s", Cp("acb", 32, 64, 0, 64), Cp("ac3", 32, 64, 64, 128), "dpb")
    dma("s", Cp("acb", 32, 64, 64, 128), Cp("ac3", 32, 64, 0, 64), "dpb")
    dma("s", Cp("acb", 0, 32, 0, 64), Cp("cc", 0, 32, 64, 128), "dpb")
    dma("s", Cp("acb", 0, 32, 64, 128), Cp("cc", 0, 32, 0, 64), "dpb")
    dma("s", Cp("keyb", 0, 64, 0, 64), Cp("key3", 0, 64, 64, 128), "dpb")
    dma("s", Cp("keyb", 0, 64, 64, 128), Cp("key3", 0, 64, 0, 64), "dpb")
    k1, k2 = 128 * slots["ac3"], 128 * slots["acb"]
    dma("s", T.cb[64:128, k2:k2 + 256], T.cb[64:128, k1:k1 + 256], "dpb")
    for a, b in (("n16r", "n16"), ("l256r", "l256a")):
        dma("s", Cs(a, 16, 0, 64), Cs(b, 16, 64, 128), "dpb", [kpl])
        dma("s", Cs(a, 16, 64, 128), Cs(b, 16, 0, 64), "dpb")

    x = act(T.W[:, 256:512], T.W[:, 0:256], [kid], bias=256.0)
    x = act(T.W[:, 512:1024], T.W[:, 0:512], [x], bias=512.0)
    i2 = act(T.W[:, 1024:2048], T.W[:, 0:1024], [x], bias=1024.0)

    P = {n: T["p%d" % n][:, 0:128] for n in (1, 2, 3, 4)}

    def place(n, parts, toks):
        mms(P[n], [(Cs(w, 16, 0, 128), Cs(q, 16, 0, 128)) for w, a, b in parts for q in (a, b)], True, False, toks)
    place(1, (("selAll", "n16", "nk"),), [sall, kn])
    place(2, (("selAll", "n16", "nk"),), [])

    n1 = cp(T.lnf[0:16, 1:33], T.ln2[0:16, :], al("lfr"))
    n2 = tt(T.hf[0:16, 1:33], T.fr[0:16, :], T.ln2[0:16, :], OP.add)
    need("v", [n1])
    n3 = tok(g.vector.tensor_tensor_scan(T.first[0:16, :], T.lnf[0:16, 0:32], T.ones[0:16, :], 0.0, OP.add, OP.mult), "cv")
    n4 = tt(T.di[0:16, :], T.fr[0:16, :], T.hf[0:16, 0:32], OP.subtract, [n2])
    n3 = cp(T.fi[0:16, :], T.first[0:16, :], [n3])

    def Q(k):
        return T.qi[0:16, 32 * k:32 * k + 32]
    ts(Q(2), T.di[0:16, :], -64, None, OP.bitwise_and, None, [n4])
    ts(Q(3), T.di[0:16, :], 63, None, OP.bitwise_and)
    ts(Q(0), T.fi[0:16, :], 15, None, OP.bitwise_and, None, [n3])
    q1 = ts(Q(1), T.fi[0:16, :], 4, None, OP.logical_shift_right)
    x = cp(T.qb[0:16, 0:128], T.qi[0:16, 0:128], [q1])

    def turn(dst, c0, ks, toks):
        need("p", toks)
        for i, k in enumerate(ks):
            for b in range(4):
                ins = g.tensor.matmul(dst[32 * b:32 * b + 32, c0 + NT * i:c0 + NT * i + NT],
                                      T.qb[0:16, 32 * k:32 * k + 32], Cs("tgs", 16, NT * b, NT * b + NT), True, True)
        return tok(ins, "cp")
    zz = turn(T.px, 0, (1, 2, 3, 0), [x, tgs])
    nl = cp(Cs("lit", 8, 0, 128), T.litr[0:8, :], al("llit"))
    for b in range(4):
        cp(*block("Gc", b, 0, 32 if b < 2 else 16))
    setup = ts(C("mc"), C("tabc"), p2b, None, OP.is_equal, None, [ktc])
    need("p", [nl])
    for k, n in enumerate(("sel0", "sel1")):
        ins = g.tensor.matmul(T.pta[:, 128 * k:128 * k + 128], Cs(n, 8, 0, 128), Cs("lit", 8, 0, 128), True, True)
    tta = tok(ins, "cp")
    act(T.W[:, ID + 2048:ID + 2176], T.pta[:, 0:128], [tta, b2], bias=code)
    act(T.W[:, S1 + 2048:S1 + 2176], T.pta[:, 0:128], bias=code)
    act(T.W[:, S2 + 2048:S2 + 2176], T.pta[:, 128:256], bias=code)
    tails = act(T.W[:, S3 + 2048:S3 + 2176], T.pta[:, 128:256], bias=code)

    def X(k, t):
        return T.px[:, NT * k + t:NT * k + t + 1]

    def Z(k, t):
        return T.zf[:, NT * k + t:NT * k + t + 1]

    def nat(n, t, m, toks, stop):
        need("v", toks)
        w = "%d%s" % (t, m)
        for h in (0, 1):
            x = ts(C("n1" + w + str(h)), C("cc"), X(0, t), X(1 + h, t), OP.is_gt, OP.mult)
            mms(P[n], [(C("m" + m), C("n1" + w + str(h)))], False, False, [x])
        ts(C("nl" + w), C("G" + m), X(3, t), None, OP.is_ge)
        for h in (0, 1):
            x = ts(C("n2" + w + str(h)), C("cc"), X(0, t), X(1 + h, t), OP.is_equal, OP.mult)
            y = mms(P[n], [(C("nl" + w), C("n2" + w + str(h)))], False, stop and h == 1, [x])
        return y

    def lst(n, t, m, row, key, toks, stop):
        need("v", toks)
        w = "%d%s" % (t, m)
        for k, (r, z, op, side, lop) in enumerate(((row, 1, OP.is_gt, "L", OP.is_lt), (row, 1, OP.is_ge, "G", OP.is_gt),
                                                   (key, 2, OP.is_ge, "G", OP.is_equal))):
            ts(C("ql%d%s" % (k, w)), C(side + m), Z(0, t), None, lop)
            for h in (0, 1):
                x = ts(C("q%d%s%d" % (k, w, h)), C(r), Z(z, t), X(1 + h, t), op, OP.mult)
                y = mms(P[n], [(C("ql%d%s" % (k, w)), C("q%d%s%d" % (k, w, h)))], False, stop and k == 2 and h == 1, [x])
        return y

    def gather(out, o0, win, w0, w1, lu, nv, toks, c0=0, c1=128):
        need("v", toks)
        cm = c0 + nv
        tv = tok(g.vector.tensor_copy(out[:, o0 + 16 * c0:o0 + 16 * cm], win[:, w0:w1].indirect(lu[:, c0:cm])), "cv")
        need("a", toks)
        ta = tok(g.scalar.activation(out[:, o0 + 16 * cm:o0 + 16 * c1], win[:, w0:w1].indirect(lu[:, cm:c1]), AF.Copy), "ca")
        return [tv, ta]

    def ship(v, src, sem, toks, q="s"):
        r, k = v // 2, v % 2
        if r == me:
            dma(q, T.y[me:me + 1, 2048 * k:2048 * k + 2048], src, "shown", toks)
        else:
            dma(q, T.ost[r:r + 1, 64 * k:64 * k + 64, :], src, sem, toks)

    def ship2(r, src, sem, toks, q="s"):
        if r == me:
            dma(q, T.y[me:me + 1, :], src, "shown", toks)
        else:
            dma(q, T.ost[r:r + 1, :, :], src, sem, toks)

    def send(c):
        trs, used = [], []
        for r in CALLS[c]:
            if r != me:
                rid, pid = topo.addr(T.cores[r])[:2]
                e = topo.engines(core, T.cores[r])
                if topo.chip(core) == topo.chip(T.cores[r]):
                    e = e[::-1]
                e = [i for i in e if i not in used][:NE]
                used.extend(e)
                trs.append(RemoteDMATransfer(dst_ids=[DstId(rid=rid, pnc=pid)], dma_engine_mask=sum(1 << i for i in e),
                                             remote_sem=T.sem.yarr, src=T.ost[r], dst=T.yland[me]))
                cnt["rloc"] += NE
        if trs:
            need("g", al("sh%d" % c))
            g.remote_dma_fused(trs, local_sem=T.sem.rloc)

    t1 = nat(1, 0, "all", [zz, gdone, kcc], True)
    ts(Q(4), Q(1), 15, None, OP.bitwise_and)
    x = ts(Q(5), T.fi[0:16, :], 4, 112, OP.logical_shift_right, OP.bitwise_and)
    x = tt(Q(6), Q(5), Q(0), OP.add, [x])
    e1 = cp(T.u1[:, :], T.p1[:, 0:128], [t1])
    x = cp(T.qb[0:16, 128:224], T.qi[0:16, 128:224], [x])
    t2 = nat(2, 1, "all", [], True)
    tz = turn(T.ptb, 128, (4, 5, 6), [x])
    place(3, (("s03", "n16", "nk"), ("s46", "n16", "nk"), ("s57", "l256", "l16")), [kl3] + al("dsel"))
    s1 = gather(T.W, S1, T.W, ID, ID + 2176, T.u1, NV[0], [e1, i2, tails])
    e2 = cp(T.u2[:, :], T.p2[:, 0:128], [t2])
    dma("s", T.u5[112:128, :], T.u1[32:48, :], "du5", [e1, fill])
    dma("s", T.u7[48:64, :], T.u1[96:112, :], "du7")
    ship(0, T.W[0:1, S1:S1 + 2048], "sh0", s1)
    dma("s", T.u6[112:128, :], T.u2[32:48, :], "du6", [e2])
    xl = cp(T.litf[:, :], T.litx[:, :], al("llx"))

    def lits(out, p, n, toks):
        need("g", toks)
        return tok(g.partition_broadcast(out, T.litf[p:p + 1, :], n), "cg")
    iota(T.W[:, ID + SYM:ID + SYM + 256], [[1, 256]], 0, 0, al("cg"))
    l5 = lits(T.W[:, ID + 2048:ID + 2176], 32, 128, [xl] + s1)
    iota(T.Y[:, Y7 + SYM:Y7 + SYM + 256], [[1, 256]], 0, 0, al("cg"))
    x = lits(T.Y[:, Y7 + 2048:Y7 + 2176], 32, 128, al("cg"))
    l6 = lits(T.Y[0:16, Y7 + 2048:Y7 + 2176], 64, 16, [x])
    iota(T.Y[:, Y11 + SYM:Y11 + SYM + 256], [[1, 256]], 0, 0, al("cg"))
    x = lits(T.Y[:, Y11 + 2048:Y11 + 2176], 0, 128, al("cg"))
    l7 = lits(T.Y[0:64, Y11 + 2048:Y11 + 2176], 96, 64, [x])
    x = cp(T.zf[:, 0:3 * NT], T.ptb[:, 128:128 + 3 * NT], [tz])
    need("v", [x])
    cp(T.zf[0:32, 3:5], T.px[0:32, 3 * NT + 3:3 * NT + 5])
    zl = cp(T.zf[0:32, NT + 3:NT + 5], T.px[0:32, 3:5])
    nat(3, 2, "c", [setup], False)
    t3 = lst(3, 5, "b1", "ac3", "key3", [zl, ablk, kk] + al("dpa"), True)
    place(4, (("s0", "n16", "nk"), ("s1", "n16r", "nk"), ("s2", "l256a", "l16a"), ("s3", "l256r", "l16a"),
              ("s46", "l256", "l16"), ("s57", "l256", "l16")), [kpl] + al("dpb"))
    s2 = gather(T.W, S2, T.W, S1, S1 + 2176, T.u2, NV[1], s1 + [e2])
    e3 = cp(T.u3[:, :], T.p3[:, 0:128], [t3])
    ship(1, T.W[0:1, S2:S2 + 2048], "sh0", s2)
    lst(4, 3, "a1", "ac3", "key3", [], False)
    t4 = lst(4, 4, "b1", "acb", "keyb", al("dpb"), True)
    s3 = gather(T.W, S3, T.W, S2, S2 + 2176, T.u3, NV[2], s2 + [e3])
    e4 = ts(T.u4[:, :], T.p4[:, 0:128], off4, None, OP.add, None, [t4])
    dma("s", T.u7[112:128, :], T.u3[32:48, :], "du7", [e3])
    dma("s", T.fl6[32:48, :], T.W[80:81, S3:S3 + 2048], "dl6", s3)
    dma("s", T.fl7[80:96, :], T.W[112:113, S3:S3 + 2048], "dl7")
    ship(2, T.W[0:1, S3:S3 + 2048], "sh0", s3)
    s4 = gather(T.W, S4, T.W, S1, S3 + 2176, T.u4, NV[3], s3 + [e4], 0, 64)
    dma("s", T.fl5[0:112, 0:64], T.W[32:39, S4:S4 + 1024], "dl5", s4)
    dma("s", T.fl5[0:112, 64:128], T.W[48:55, S4:S4 + 1024], "dl5")
    dma("s", T.W[0:128:16, ID:ID + 1024], T.W[0:8, S4:S4 + 1024], "dy3")
    dma("s", T.W[0:128:16, ID + 1024:ID + 2048], T.W[16:24, S4:S4 + 1024], "dy3")
    s4 = gather(T.W, S4, T.W, S1, S3 + 2176, T.u4, NV[4], s3 + [e4], 64, 128)
    f1 = cp(T.f1[64:96, :], T.u1[64:96, :])
    dma("s", T.fl6[48:112, :], T.W[64:68, S4:S4 + 2048], "dl6", s4)
    dma("s", T.fl6[16:32, :], T.W[80:81, S4:S4 + 2048], "dl6")
    dma("s", T.fl6[0:16, :], T.f1[64:80, :], "dl6", [f1])
    dma("s", T.fl7[64:80, :], T.W[112:113, S4:S4 + 2048], "dl7")
    dma("s", T.fl7[96:112, :], T.W[96:97, S4:S4 + 2048], "dl7")
    ship(3, T.W[0:1, S4:S4 + 2048], "sh0", s4)
    e5 = cp(T.u5[0:112, :], T.fl5[0:112, :], al("dl5"))
    s5 = gather(T.Y, Y7, T.W, ID, ID + 2432, T.u5, NV[5], al("dy3", "du5") + [e5, l5])
    e6 = cp(T.u6[0:112, :], T.fl6[0:112, :], al("dl6"))
    ship(4, T.Y[112:113, Y7:Y7 + 2048], "sh1", s5)
    ship(7, T.Y[0:1, Y7:Y7 + 2048], "sh2", s5)
    s6 = gather(T.Y, Y11, T.Y, Y7, Y7 + 2432, T.u6, NV[6], s5 + al("du6") + [e6, l6])
    e7 = cp(T.u7[64:112, :], T.fl7[64:112, :], al("dl7"))
    ship2(4, T.Y[0:32:16, Y11:Y11 + 2048], "sh1", s6)
    ship2(5, T.Y[32:64:16, Y11:Y11 + 2048], "sh1", s6)
    ship(5, T.Y[112:113, Y11:Y11 + 2048], "sh1", s6)
    s7 = gather(T.Y, YF, T.Y, Y11, Y11 + 2432, T.u7, NV[7], s6 + al("du7") + [e7, l7])
    ship2(6, T.Y[48:80:16, YF:YF + 2048], "sh2", s7)
    ship2(7, T.Y[80:112:16, YF:YF + 2048], "sh2", s7, "a")
    ship(6, T.Y[112:113, YF:YF + 2048], "sh2", s7)
    for c in range(3):
        send(c)
    cnt["yarr"] = 7 * NE
    if me > 0:
        dma("s", T.y[0:me, :], T.yland[0:me, :, :], "yst", al("yarr"))
    if me < 7:
        dma("a", T.y[me + 1:8, :], T.yland[me + 1:8, :, :], "yst", al("yarr"))
    for s in list(cnt):
        if max([v for (q, n), v in seen.items() if n == s] + [0]) < cnt[s]:
            need("g", [(s, cnt[s])])
